import numpy as np, ml_dtypes
CORES = [24,25,26,27,28,29,30,31]
N = 8
import mx_ref
BF = ml_dtypes.bfloat16
def entries(a):
    return np.ascontiguousarray(a.T).reshape(-1)
def table(e):
    return np.ascontiguousarray(np.reshape(e, (-1, 16)).T).astype(np.int32)
def cols(t, e):
    v = np.concatenate([t.reshape(128, -1, 4), np.zeros((128, 1, 4), BF)], axis=1)
    return np.ascontiguousarray(v[:, e]).reshape(128, -1)
def cut(t, i, w=512):
    return t[:, w * i:w * i + w]
def f(rng, *shape):
    return mx_ref.flush((rng.standard_normal(shape, dtype=np.float32) * np.exp2(rng.integers(-2, 3, shape[:-1] + (1,)))).astype(BF))
def wide(rng, *shape, cols=0):
    v = rng.standard_normal(shape, dtype=np.float32) * np.exp2(rng.integers(-12, 13, shape)).astype(np.float32)
    if cols: v *= np.repeat(np.exp2(rng.integers(-cols, cols + 1, shape[:-2] + (1, shape[-1] // 4))) * (rng.random(shape[:-2] + (1, shape[-1] // 4)) > 0.0625), 4, axis=-1).astype(np.float32)
    return mx_ref.flush(v.astype(BF))
TB, T, CAPP, O = 512, 512, 48, 1
def lists(rng, case=""):
    o = []; odd = rng.permutation(N)
    for r in range(N):
        lo, hi = {"one": (1, 1), "full": (CAPP, CAPP), "runs": (1, CAPP // 2), "none": (1, CAPP)}.get(case, (0, CAPP))
        n = rng.integers(lo, hi + 1, N)
        if case == "none":
            if r == odd[0]: n[:] = 0; n[rng.integers(0, N)] = 1
            elif r == odd[1]: n[r] = 0
            elif r == odd[2]: n[np.arange(N) != r] = 0
            else: n[rng.permutation(N)[:rng.integers(1, N)]] = 0
        if n.sum() == 0: n[rng.integers(0, N)] = 1
        if case == "full": named = [np.append([0, TB - 1], 1 + rng.permutation(TB - 2)[:n[q] - 2]) for q in range(N)]
        else: named = [rng.permutation(TB)[:n[q]] for q in range(N)]
        pool = rng.permutation(np.concatenate([q * TB + named[q] for q in range(N)]))
        i = np.arange(len(pool))
        k = T - len(pool)
        i = np.concatenate([i, (rng.random(k) * rng.random(k) * len(pool)).astype(int)])
        i = np.sort(i) if case == "runs" else rng.permutation(i)
        o.append(table(pool[i]))
    return {"want": np.stack(o)}
def setup_inputs(rng):
    return {"x": f(rng, N, 128, 4 * TB), "w": f(rng, N, 128, 512 * O), **lists(rng)}
def setup_inputs_one(rng):
    return {**setup_inputs(rng), **lists(rng, "one")}
def setup_inputs_full(rng):
    return {**setup_inputs(rng), **lists(rng, "full")}
def setup_inputs_runs(rng):
    return {**setup_inputs(rng), **lists(rng, "runs")}
def setup_inputs_none(rng):
    return {**setup_inputs(rng), **lists(rng, "none")}
def setup_inputs_spread(rng):
    d = setup_inputs(rng); d["x"] = wide(rng, N, 128, 4 * TB, cols=8); return d
def check_inputs(d):
    b = []
    for r in range(N):
        e = entries(d["want"][r])
        if e.min() < 0 or e.max() >= N * TB or any(len(np.unique(e[e // TB == q])) > CAPP for q in range(N)): b.append("want")
    return b
def reference(x, w, want):
    every = np.concatenate([x[q] for q in range(N)], axis=1)
    y = np.zeros((N, 128, O * T), np.float32)
    for r in range(N):
        t = mx_ref.quantize(cols(every, entries(want[r])))
        for o in range(O):
            y[r][:, T * o:T * o + T] = mx_ref.matmul(mx_ref.quantize(np.ascontiguousarray(cut(w[r], o))), t)
    return {"y": y}

@@ -1,0 +1,322 @@
+from concourse.bass import DstId, RemoteDMATransfer
+from concourse.mybir import dt, AluOpType, AxisListType, ActivationFunctionType
+
+A = AluOpType
+F = ActivationFunctionType
+CAP = 48
+PL = 528
+BIG = 8192.0
+
+SCRATCH = {
+    "Lw": ("sbuf", [128, 32], "int32"), "C": ("sbuf", [128, 4], "int32"), "Cf": ("sbuf", [128, 4], "float32"),
+    "Cb": ("sbuf", [128, 4], "float32"),
+    "off0": ("sbuf", [128, 32], "uint16"), "Tab": ("sbuf", [128, 4096], "float32"),
+    "R16": ("sbuf", [128, 384], "uint16"), "RS": ("sbuf", [128, 128], "float32"),
+    "E0": ("sbuf", [128, 512], "bfloat16"), "E1": ("sbuf", [128, 384], "bfloat16"),
+    "E2": ("sbuf", [128, 256], "bfloat16"), "E3": ("sbuf", [128, 128], "bfloat16"),
+    "NB": ("sbuf", [128, 2048], "bfloat16"),
+    "M": ("sbuf", [128, 512], "bfloat16"), "ones": ("sbuf", [128, 256], "bfloat16"),
+    "pid": ("sbuf", [128, 1], "int32"), "p4": ("sbuf", [128, 1], "int32"), "p3": ("sbuf", [128, 1], "int32"),
+    "xp0": ("sbuf", [128, 1], "float32"), "xp": ("sbuf", [128, 1], "float32"), "t2": ("sbuf", [128, 1], "float32"),
+    "gsh": ("sbuf", [128, 1], "float32"), "gsh2": ("sbuf", [128, 1], "float32"),
+    "did": ("sbuf", [128, 4], "float32"), "k16": ("sbuf", [128, 4], "float32"), "thr": ("sbuf", [128, 4], "float32"),
+    "K": ("sbuf", [128, 4], "float32"), "G": ("sbuf", [128, 40], "float32"), "TG": ("sbuf", [128, 32], "float32"),
+    "off1": ("sbuf", [128, 16], "uint16"), "Win": ("sbuf", [128, 8704], "bfloat16"),
+    "OB": ("sbuf", [128, 512], "bfloat16"),
+    "CW": ("sbuf", [128, 544], "bfloat16"), "J0": ("sbuf", [128, 512], "float32"), "J1": ("sbuf", [128, 512], "float32"),
+    "J2": ("sbuf", [128, 512], "bfloat16"),
+    "LR": ("sbuf", [128, 32], "float32"), "X1": ("sbuf", [128, 32], "float32"), "X3": ("sbuf", [128, 32], "float32"),
+    "O": ("sbuf", [128, 24], "uint16"),
+    "x0": ("sbuf", [128, 2048], "bfloat16"), "XP": ("sbuf", [128, 4 * PL], "bfloat16"),
+    "wt": ("sbuf", [128, 512], "bfloat16"),
+    "HA": ("sbuf", [128, 768], "bfloat16"), "HB": ("sbuf", [128, 768], "bfloat16"),
+    "QA": ("sbuf", [128, 192], "float8_e4m3fn_x4"), "QB": ("sbuf", [128, 192], "float8_e4m3fn_x4"),
+    "SA": ("sbuf", [128, 192], "uint8"), "SB": ("sbuf", [128, 192], "uint8"),
+    "QW": ("sbuf", [128, 128], "float8_e4m3fn_x4"), "SW": ("sbuf", [128, 128], "uint8"),
+    "CR": ("sbuf", [128, 336], "float8_e4m3fn_x4"), "SR": ("sbuf", [128, 336], "uint8"),
+    "pa": ("psum", [128, 512], "float32"), "pb": ("psum", [128, 512], "float32"), "po": ("psum", [128, 512], "float32"),
+    "Z": ("sbuf", [128, 384], "float32"), "yv": ("sbuf", [128, 256], "float32"), "ys": ("sbuf", [128, 256], "float32"),
+    "o1": ("sbuf", [128, 32], "float32"), "OP": ("sbuf", [128, 64], "uint16"),
+    "q1": ("sbuf", [128, 32], "int32"), "q2": ("sbuf", [128, 32], "int32"), "q3": ("sbuf", [128, 32], "int32"),
+    "q4": ("sbuf", [128, 32], "float32"),
+    "Pr": ("sbuf", [128, 1024], "bfloat16"), "PT": ("sbuf", [128, 1024], "bfloat16"),
+    "xa": ("sbuf", [128, 32], "float32"), "xb": ("sbuf", [128, 32], "float32"), "xc": ("sbuf", [128, 32], "float32"),
+    "xd": ("sbuf", [128, 32], "float32"), "xe": ("sbuf", [128, 32], "float32"), "xf": ("sbuf", [128, 32], "float32"),
+    "FO": ("sbuf", [128, 32], "uint16"),
+}
+SEMAPHORES = ["v", "s", "g", "t", "lw", "lc", "lx", "lv", "ly", "la", "aa", "ab", "out"]
+
+
+def rank_program(g, core, T, topo):
+    r = T.rank_of(core)
+    if r is None:
+        return
+    N = len(T.cores)
+    S = T.sem
+    cnt = {"v": 0, "s": 0, "g": 0, "t": 0}
+    queues = {"v": g.vector, "s": g.scalar, "g": g, "t": g.tensor, "y": g.sync}
+    waited = {}
+
+    def need(qn, *toks):
+        for name, n in toks:
+            if waited.get((qn, name), 0) < n:
+                waited[(qn, name)] = n
+                queues[qn].wait_ge(S[name], n)
+
+    def done(qn, ins):
+        ins.then_inc(S[qn], 1)
+        cnt[qn] += 1
+        return (qn, cnt[qn])
+
+    V, Sc = g.vector, g.scalar
+
+    for h in range(8):
+        q = g.sync if h % 2 == 0 else g.scalar
+        q.dma_start(T.Lw[16 * h:16 * h + 16, :], T.want[:, :]).then_inc(S.lw, 16)
+    for k in range(4):
+        q = g.sync if k % 2 == 0 else g.scalar
+        q.dma_start(T.C[:, k:k + 1], T.want[:, 8 * k:8 * k + 8]).then_inc(S.lc, 16)
+    g.sync.dma_start(T.x0[:, :], T.x[:, :]).then_inc(S.lx, 16)
+    g.sync.dma_start(T.wt[:, :], T.w[:, :]).then_inc(S.lv, 16)
+
+    kPid = done("g", g.iota(T.pid[:, :], [[1, 1]], 0, 1))
+    kTabG = done("g", g.iota(T.Tab[:, 3104:4096], [[1, 992]], 3104, 0, allow_small_or_imprecise_dtypes=True))
+    kDid = done("g", g.iota(T.did[:, :], [[1, 4]], 4096, 4, allow_small_or_imprecise_dtypes=True))
+    kK16 = done("g", g.iota(T.k16[:, :], [[16, 4]], 0, 1, allow_small_or_imprecise_dtypes=True))
+    kOnes = done("v", V.memset(T.ones[:, :], 1.0))
+    need("v", kOnes)
+    tV0 = done("v", V.tensor_tensor_scan(T.Tab[:, 0:256], T.ones[:, :], T.ones[:, :], -1.0, A.add, A.mult))
+    need("v", kPid)
+    kP4 = done("v", V.tensor_scalar(T.p4[:, :], T.pid[:, :], 4, None, A.arith_shift_right))
+    kP3 = done("v", V.tensor_scalar(T.p3[:, :], T.pid[:, :], 3, None, A.arith_shift_right))
+    need("v", tV0)
+    tV1 = done("v", V.tensor_scalar(T.Tab[:, 256:512], T.Tab[:, 0:256], 256.0, None, A.add))
+    need("v", kP3)
+    kX0 = done("v", V.tensor_scalar(T.xp0[:, :], T.p3[:, :], -127.0, None, A.mult))
+    need("v", tV1)
+    tV2 = done("v", V.tensor_scalar(T.Tab[:, 512:1024], T.Tab[:, 0:512], 512.0, None, A.add))
+    tV3 = done("v", V.tensor_scalar(T.Tab[:, 1024:1312], T.Tab[:, 0:288], 1024.0, None, A.add))
+    kWin = done("v", V.memset(T.Win[:, 4096:4608], 0.0))
+    need("v", kX0)
+    kXp = done("v", V.tensor_scalar(T.xp[:, :], T.pid[:, :], 16.0, T.xp0[:, 0:1], A.mult, A.add))
+    kM = done("v", V.memset(T.M[:, 128:512], 0.0))
+    need("v", kXp)
+    kTri = done("v", V.tensor_scalar(T.M[:, 0:128], T.Tab[:, 0:128], T.xp[:, 0:1], BIG, A.is_le, A.mult))
+    need("s", tV0)
+    done("s", Sc.activation(T.Tab[:, 1312:1568], T.Tab[:, 0:256], F.Identity, bias=1312.0))
+    need("s", tV1)
+    done("s", Sc.activation(T.Tab[:, 1568:2080], T.Tab[:, 0:512], F.Identity, bias=1568.0))
+    need("s", tV2)
+    tS = done("s", Sc.activation(T.Tab[:, 2080:3104], T.Tab[:, 0:1024], F.Identity, bias=2080.0))
+
+    need("v", ("lw", 128))
+    kOff0 = done("v", V.tensor_copy(T.off0[:, :], T.Lw[:, :]))
+    need("v", ("lc", 64))
+    kCb = done("v", V.tensor_scalar(T.Cb[:, :], T.C[:, :], BIG, None, A.mult))
+    need("v", kOff0, tS, kTabG)
+    kR = done("v", V.tensor_copy(T.R16[:, :], T.Tab[:, 0:4096].indirect(T.off0[:, 0:24])))
+    kC = done("v", V.tensor_copy(T.Cf[:, :], T.C[:, :]))
+    need("s", kOff0, tV3, tS, kTabG)
+    kRS = done("s", Sc.activation(T.RS[:, :], T.Tab[:, 0:4096].indirect(T.off0[:, 24:32]), F.Copy))
+    E = [T.E0, T.E1, T.E2, T.E3]
+    need("s", kRS, kCb)
+    kS = [done("s", Sc.activation(E[k][:, 384 - 128 * k:512 - 128 * k], T.RS[:, :], F.Abs, bias=T.Cb[:, k:k + 1], scale=-BIG)) for k in range(4)]
+    need("v", kR, kC)
+    kE = [done("v", V.tensor_scalar(E[k][:, 0:384 - 128 * k], T.R16[:, 128 * k:384], T.Cf[:, k:k + 1], BIG, A.not_equal, A.mult)) for k in range(3)]
+    need("v", kTri, kM)
+    for k in range(4):
+        need("v", kS[k])
+        if k < 3:
+            need("v", kE[k])
+        kN = done("v", V.tensor_tensor_scan(T.NB[:, 640 * k:512 * k + 512], E[k][:, :], T.M[:, 0:512 - 128 * k], BIG, A.min, A.max))
+    need("s", kWin)
+    done("s", Sc.activation(T.Win[:, 2048:2560], T.Win[:, 4096:4608], F.Copy))
+    kWin2 = done("s", Sc.activation(T.Win[:, 6144:6656], T.Win[:, 4096:4608], F.Copy))
+    need("v", kN, kDid)
+    kK = done("v", V.tensor_tensor(T.K[:, :], T.did[:, :], T.NB[:, 511:2048:512], A.subtract))
+    need("v", kK)
+    e1 = done("v", V.tensor_tensor(T.G[:, 0:4], T.K[:, :], T.Cf[:, :], A.max))
+    e2 = done("v", V.tensor_tensor(T.G[:, 12:16], T.K[:, :], T.Cf[:, :], A.max))
+    need("v", e1)
+    need("s", e1)
+    done("v", V.tensor_copy(T.G[0:64, 4:8], T.G[64:128, 0:4]))
+    a1 = done("v", V.tensor_copy(T.G[0:64, 8:12], T.G[64:128, 0:4]))
+    done("s", Sc.activation(T.G[64:128, 4:8], T.G[0:64, 0:4], F.Copy))
+    b1 = done("s", Sc.activation(T.G[64:128, 8:12], T.G[0:64, 0:4], F.Copy))
+    kGsh = done("v", V.tensor_scalar(T.gsh[:, :], T.p4[:, :], -512.0, 4096.0, A.mult, A.add))
+    need("v", a1, b1, e2)
+    need("s", a1, b1)
+    done("v", V.tensor_copy(T.G[0:32, 16:32], T.G[32:64, 0:16]))
+    done("v", V.tensor_copy(T.G[32:64, 16:32], T.G[0:32, 0:16]))
+    a2 = done("v", V.tensor_copy(T.G[:, 32:40], T.G[:, 0:8]))
+    done("s", Sc.activation(T.G[64:96, 16:32], T.G[96:128, 0:16], F.Copy))
+    b2 = done("s", Sc.activation(T.G[96:128, 16:32], T.G[64:96, 0:16], F.Copy))
+    kT2 = done("v", V.tensor_scalar(T.t2[:, :], T.p4[:, :], -16.0, 0.5, A.mult, A.add))
+    need("v", a2, b2)
+    kTG = done("v", V.transpose(T.TG[:, :], T.G[:, 8:40]))
+    need("v", kTG, kGsh)
+    done("v", V.tensor_scalar(T.off1[0:64, :], T.TG[0:64, 0:16], T.gsh[0:64, 0:1], None, A.add))
+    kO1 = done("v", V.tensor_scalar(T.off1[64:128, :], T.TG[64:128, 16:32], T.gsh[64:128, 0:1], None, A.add))
+    need("v", kT2, kK16)
+    kThr = done("v", V.tensor_scalar(T.thr[:, :], T.k16[:, :], T.t2[:, 0:1], None, A.add))
+    need("v", kO1, kWin, kWin2)
+    kSc = done("v", V.tensor_copy(T.Win[:, 0:8704].indirect(T.off1[:, 0:16]), T.ones[:, :]))
+    need("v", kSc)
+    need("s", kSc)
+    done("v", V.tensor_copy(T.OB[0:64, :], T.Win[64:128, 2048:2560]))
+    o1 = done("v", V.tensor_copy(T.OB[64:128, 0:160], T.Win[0:64, 6144:6304]))
+    o2 = done("s", Sc.activation(T.OB[64:128, 160:512], T.Win[0:64, 6304:6656], F.Copy))
+    need("v", o1, o2)
+    kCum = done("v", V.tensor_tensor_scan(T.CW[:, 16:528], T.Win[:, 4096:4608], T.OB[:, :], 0.0, A.add, A.add))
+    need("s", kCum, kThr)
+    done("s", Sc.activation(T.J0[:, :], T.CW[:, 16:528], F.Sign, bias=T.thr[:, 0:1], scale=-1.0, accum_out=T.LR[:, 28:29]))
+    c1 = done("s", Sc.activation(T.J1[:, :], T.CW[:, 16:528], F.Sign, bias=T.thr[:, 1:2], scale=-1.0, accum_out=T.LR[:, 29:30]))
+    need("v", kCum, kThr)
+    kJ2 = done("v", V.tensor_scalar(T.J2[:, :], T.CW[:, 16:528], T.thr[:, 2:3], None, A.is_lt))
+    z3 = done("v", V.memset(T.LR[:, 31:32], 0.0))
+    need("v", kJ2)
+    c2 = done("v", V.tensor_reduce(T.LR[:, 30:31], T.J2[:, :], AxisListType.X, A.add))
+    sent = [0]
+
+    def fused(items):
+        tr = []
+        for dst, src, out, sem, eng in items:
+            dc = T.cores[dst]
+            rid, pid, _ = topo.addr(dc)
+            es = topo.engines(core, dc)
+            m = 0
+            for j in eng(len(es)):
+                m |= 1 << es[j]
+                sent[0] += 1
+            tr.append(RemoteDMATransfer(dst_ids=[DstId(rid=rid, pnc=pid)], dma_engine_mask=m, remote_sem=sem, src=src, dst=out))
+        g.remote_dma_fused(tr, local_sem=S.out)
+
+    def every(i, n):
+        return lambda ne: range(i, ne, n)
+
+    need("g", c1, z3, c2)
+    fused([((r - 1 - i) % N, T.LR[:, 28:32], T.LR[:, 4 * i:4 * i + 4], S.la, every(i, 8)) for i in range(7)])
+
+    need("v", ("lx", 16))
+    for t in (0, 1):
+        kPlV = done("v", V.tensor_copy(T.XP[:, PL * t:PL * t + 512], T.x0[:, t:2048:4]))
+    for t in range(4):
+        kPad = done("v", V.memset(T.XP[:, PL * t + 512:PL * t + 528], 0.0))
+    need("s", ("lx", 16))
+    for t in (2, 3):
+        kPlS = done("s", Sc.activation(T.XP[:, PL * t:PL * t + 512], T.x0[:, t:2048:4], F.Copy))
+    kGsh2 = done("v", V.tensor_scalar(T.gsh2[:, :], T.p4[:, :], -512.0, 16.0, A.mult, A.add))
+    need("v", ("lv", 16))
+    kW = done("v", V.quantize_mx(T.QW[:, :], T.SW[:, :], T.wt[:, :]))
+    need("v", kGsh2)
+    ko1 = done("v", V.tensor_scalar(T.o1[:, :], T.Lw[:, :], T.gsh2[:, 0:1], 528.0, A.add, A.min))
+    kq1 = done("v", V.tensor_scalar(T.q1[:, :], T.Lw[:, :], 9, None, A.arith_shift_right))
+    done("v", V.memset(T.CW[:, 0:16], 0.0))
+    kCz = done("v", V.memset(T.CW[:, 528:544], 0.0))
+    need("v", ko1)
+    done("v", V.tensor_scalar(T.OP[:, 0:64:2], T.o1[:, :], 15.0, None, A.max))
+    kOP = done("v", V.tensor_scalar(T.OP[:, 1:64:2], T.o1[:, :], 15.0, None, A.max))
+    need("v", kq1)
+    kq2 = done("v", V.tensor_scalar(T.q2[:, :], T.q1[:, :], -1.0, float(r + 7), A.mult, A.add))
+    need("v", kq2)
+    kq3 = done("v", V.tensor_scalar(T.q3[:, :], T.q2[:, :], 7, None, A.bitwise_and))
+    need("v", kq3)
+    kq4 = done("v", V.tensor_scalar(T.q4[:, :], T.q3[:, :], 48.0, -1.0, A.mult, A.add))
+
+    a, b = divmod(r, 2)
+    ra = slice(32 * a, 32 * a + 32)
+    hb = slice(16 * b, 16 * b + 16)
+    need("v", ("la", 14), c1, c2)
+    kX1 = done("v", V.transpose(T.X1[ra, :], T.LR[ra, :]))
+    need("v", kX1)
+    need("s", kX1)
+    todo = [(d, u) for d in range(4) for u in range(2) if (d, u) != (a, b)]
+    kcs = kcv = None
+    for n, (d, u) in enumerate(todo):
+        o = T.X1[32 * d:32 * d + 32, 16 * u:16 * u + 16]
+        if n < 3:
+            kcs = done("s", Sc.activation(o, T.X1[ra, hb], F.Copy))
+        else:
+            kcv = done("v", V.tensor_copy(o, T.X1[ra, hb]))
+    need("v", kcs, kcv)
+    kX3 = done("v", V.transpose(T.X3[:, :], T.X1[:, :]))
+    need("v", kX3)
+    done("v", V.tensor_scalar(T.O[:, 0:24:3], T.X3[:, 0:32:4], 0.5, 256.0, A.mult, A.add))
+    done("v", V.tensor_scalar(T.O[:, 1:24:3], T.X3[:, 1:32:4], 0.5, 256.0, A.mult, A.add))
+    kO = done("v", V.tensor_copy(T.O[:, 2:24:3], T.X3[:, 2:32:4]))
+    need("s", kO, kPlS, kPad)
+    kh = {}
+    for nm, H, c in (("A", T.HA, 0), ("B", T.HB, 12)):
+        for t in (2, 3):
+            kh[nm] = done("s", Sc.activation(H[:, t:768:4], T.XP[:, PL * t:PL * t + 513].indirect(T.O[:, c:c + 12]), F.Copy))
+    need("v", kO, kPlV, kPad)
+    kq = {}
+    for nm, H, c, Q, P in (("A", T.HA, 0, T.QA, T.SA), ("B", T.HB, 12, T.QB, T.SB)):
+        for t in (0, 1):
+            kv = done("v", V.tensor_copy(H[:, t:768:4], T.XP[:, PL * t:PL * t + 513].indirect(T.O[:, c:c + 12])))
+        need("v", kv, kh[nm])
+        kq[nm] = done("v", V.quantize_mx(Q[:, :], P[:, :], H[:, :]))
+
+    def codes(q, lo):
+        return q[:, lo:lo + CAP].bitcast(dt.uint8)
+
+    need("g", kq["A"])
+    fused([((r + 1 + i) % N, codes(T.QA, 48 * i), codes(T.CR, 48 * i), S.aa, every(i, 4)) for i in range(4)])
+    fused([((r + 1 + i) % N, T.SA[:, 48 * i:48 * i + 48], T.SR[:, 48 * i:48 * i + 48], S.aa, every(i, 4)) for i in range(4)])
+    need("g", kq["B"])
+    half = [every(0, 2), every(1, 4), every(3, 4)]
+    flip = [every(1, 2), every(0, 4), every(2, 4)]
+    fused([((r + 5 + i) % N, codes(T.QB, 48 * i), codes(T.CR, 192 + 48 * i), S.ab, half[i]) for i in range(3)])
+    fused([((r + 5 + i) % N, T.SB[:, 48 * i:48 * i + 48], T.SR[:, 192 + 48 * i:240 + 48 * i], S.ab, flip[i]) for i in range(3)])
+
+    ts = g.tensor
+    need("t", kW, kq["B"])
+    m0 = done("t", ts.matmul_mx(T.po[:, 0:128], T.QW[:, :], T.SW[:, :], T.QB[:, 64:192], T.SB[:, 64:192], True, True))
+    need("t", ("aa", 32))
+    m1 = done("t", ts.matmul_mx(T.pa[:, 0:192], T.QW[:, :], T.SW[:, :], T.CR[:, 0:192], T.SR[:, 0:192], True, True))
+    need("t", ("ab", 32))
+    m2 = done("t", ts.matmul_mx(T.pb[:, 0:144], T.QW[:, :], T.SW[:, :], T.CR[:, 192:336], T.SR[:, 192:336], True, True))
+
+    need("s", kOP, kCz, kCum)
+    kPs = done("s", Sc.activation(T.Pr[:, 512:1024], T.CW[:, 0:544].indirect(T.OP[:, 32:64]), F.Copy))
+    need("v", kOP, kCz, kCum)
+    kPv = done("v", V.tensor_copy(T.Pr[:, 0:512], T.CW[:, 0:544].indirect(T.OP[:, 0:32])))
+    need("v", kPs, kPv)
+    kPT = done("v", V.transpose(T.PT[:, :], T.Pr[:, :]))
+    need("v", kPT)
+    kxa = done("v", V.tensor_tensor(T.xa[:, :], T.PT[:, 0:1024:32], T.PT[:, 16:1024:32], A.add))
+    need("v", kxa)
+    need("s", kxa)
+    x1 = done("v", V.tensor_copy(T.xb[0:64, :], T.xa[64:128, :]))
+    x2 = done("s", Sc.activation(T.xb[64:128, :], T.xa[0:64, :], F.Copy))
+    need("v", x1, x2)
+    kxc = done("v", V.tensor_tensor(T.xc[:, :], T.xa[:, :], T.xb[:, :], A.add))
+    need("v", kxc, kq4)
+    need("s", kxc)
+    done("v", V.tensor_copy(T.xd[0:32, :], T.xc[32:64, :]))
+    x3 = done("v", V.tensor_copy(T.xd[32:64, :], T.xc[0:32, :]))
+    done("s", Sc.activation(T.xd[64:96, :], T.xc[96:128, :], F.Copy))
+    x4 = done("s", Sc.activation(T.xd[96:128, :], T.xc[64:96, :], F.Copy))
+    kxe = done("v", V.tensor_tensor(T.xe[:, :], T.xc[:, :], T.q4[:, :], A.add))
+    need("v", x3, x4, kxe)
+    kxf = done("v", V.tensor_tensor(T.xf[:, :], T.xe[:, :], T.xd[:, :], A.add))
+    need("v", kxf)
+    kFO = done("v", V.tensor_copy(T.FO[:, :], T.xf[:, :]))
+
+    need("v", m0)
+    zo = done("v", V.tensor_copy(T.Z[:, 336:384], T.po[:, 80:128]))
+    need("s", m1)
+    za = done("s", Sc.activation(T.Z[:, 0:192], T.pa[:, 0:192], F.Copy))
+    need("v", m2)
+    zb = done("v", V.tensor_copy(T.Z[:, 192:336], T.pb[:, 0:144]))
+    need("v", kFO, zo, za, zb)
+    yv = done("v", V.tensor_copy(T.yv[:, :], T.Z[:, 0:384].indirect(T.FO[:, 0:16])))
+    need("s", kFO, zo, za, zb)
+    ysc = done("s", Sc.activation(T.ys[:, :], T.Z[:, 0:384].indirect(T.FO[:, 16:32]), F.Copy))
+    need("y", yv)
+    g.sync.dma_start(T.y[:, 0:256], T.yv[:, :]).then_inc(S.ly, 16)
+    need("s", ysc)
+    g.scalar.dma_start(T.y[:, 256:512], T.ys[:, :]).then_inc(S.ly, 16)
+
+    need("g", ("out", sent[0]), ("v", cnt["v"]), ("s", cnt["s"]), ("g", cnt["g"]), ("t", cnt["t"]))
+    need("g", ("lw", 128), ("lc", 64), ("lx", 16), ("lv", 16), ("ly", 32), ("la", 14), ("aa", 32), ("ab", 32))

@@ -7,44 +7,23 @@ CAP = 48
 PL = 528
 BIG = 8192.0
 
+
+def sb(kind, **widths):
+    return {k: ("sbuf", [128, n], kind) for k, n in widths.items()}
+
+
 SCRATCH = {
-    "Lw": ("sbuf", [128, 32], "int32"), "C": ("sbuf", [128, 4], "int32"), "Cf": ("sbuf", [128, 4], "float32"),
-    "Cb": ("sbuf", [128, 4], "float32"),
-    "off0": ("sbuf", [128, 32], "uint16"), "Tab": ("sbuf", [128, 4096], "float32"),
-    "R16": ("sbuf", [128, 384], "uint16"), "RS": ("sbuf", [128, 128], "float32"),
-    "E0": ("sbuf", [128, 512], "bfloat16"), "E1": ("sbuf", [128, 384], "bfloat16"),
-    "E2": ("sbuf", [128, 256], "bfloat16"), "E3": ("sbuf", [128, 128], "bfloat16"),
-    "NB": ("sbuf", [128, 2048], "bfloat16"),
-    "M": ("sbuf", [128, 512], "bfloat16"), "ones": ("sbuf", [128, 256], "bfloat16"),
-    "pid": ("sbuf", [128, 1], "int32"), "p4": ("sbuf", [128, 1], "int32"), "p3": ("sbuf", [128, 1], "int32"),
-    "xp0": ("sbuf", [128, 1], "float32"), "xp": ("sbuf", [128, 1], "float32"), "t2": ("sbuf", [128, 1], "float32"),
-    "gsh": ("sbuf", [128, 1], "float32"), "gsh2": ("sbuf", [128, 1], "float32"),
-    "did": ("sbuf", [128, 4], "float32"), "k16": ("sbuf", [128, 4], "float32"), "thr": ("sbuf", [128, 4], "float32"),
-    "K": ("sbuf", [128, 4], "float32"), "G": ("sbuf", [128, 40], "float32"), "TG": ("sbuf", [128, 32], "float32"),
-    "off1": ("sbuf", [128, 16], "uint16"), "Win": ("sbuf", [128, 8704], "bfloat16"),
-    "OB": ("sbuf", [128, 512], "bfloat16"),
-    "CW": ("sbuf", [128, 544], "bfloat16"), "J0": ("sbuf", [128, 512], "float32"), "J1": ("sbuf", [128, 512], "float32"),
-    "J2": ("sbuf", [128, 512], "bfloat16"),
-    "LR": ("sbuf", [128, 32], "float32"), "X1": ("sbuf", [128, 32], "float32"), "X3": ("sbuf", [128, 32], "float32"),
-    "O": ("sbuf", [128, 24], "uint16"),
-    "x0": ("sbuf", [128, 2048], "bfloat16"), "XP": ("sbuf", [128, 4 * PL], "bfloat16"),
-    "wt": ("sbuf", [128, 512], "bfloat16"),
-    "HA": ("sbuf", [128, 768], "bfloat16"), "HB": ("sbuf", [128, 768], "bfloat16"),
-    "QA": ("sbuf", [128, 192], "float8_e4m3fn_x4"), "QB": ("sbuf", [128, 192], "float8_e4m3fn_x4"),
-    "SA": ("sbuf", [128, 192], "uint8"), "SB": ("sbuf", [128, 192], "uint8"),
-    "QW": ("sbuf", [128, 128], "float8_e4m3fn_x4"), "SW": ("sbuf", [128, 128], "uint8"),
-    "CR": ("sbuf", [128, 336], "float8_e4m3fn_x4"), "SR": ("sbuf", [128, 336], "uint8"),
+    **sb("int32", Lw=32, C=4, pid=1, p4=1, p3=1, q0=32, q1=32, q2=32, q3=32),
+    **sb("uint16", off0=32, R16=320, off1=16, O=24, OO=4, OP=64, FO=32),
+    **sb("float32", Cf=4, Cb=4, Tab=4096, RS=192, xp0=1, xp=1, t2=1, gsh=1, did=4, k16=4, thr=4, K=4, G=40, TG=32,
+         J0=512, J1=512, LR=32, X1=32, X3=32, Z=384, yv=256, ys=256, o1=32, q4=32, xa=32, xb=32, xc=32, xd=32, xe=32, xf=32),
+    **sb("bfloat16", E0=512, E1=384, E2=256, E3=128, NB=2048, ones=256, Win=8704, OB=512, CW=544, J2=512,
+         x0=2048, XP=4 * PL, wt=512, H=1344, HO=512, Pr=1024, PT=1024),
+    **sb("float8_e4m3fn_x4", Q=256, Q2=128, QO=128, QW=128, CR=336),
+    **sb("uint8", SQ=256, S2=128, SO=128, SW=128, SR=336),
     "pa": ("psum", [128, 512], "float32"), "pb": ("psum", [128, 512], "float32"), "po": ("psum", [128, 512], "float32"),
-    "Z": ("sbuf", [128, 384], "float32"), "yv": ("sbuf", [128, 256], "float32"), "ys": ("sbuf", [128, 256], "float32"),
-    "o1": ("sbuf", [128, 32], "float32"), "OP": ("sbuf", [128, 64], "uint16"),
-    "q1": ("sbuf", [128, 32], "int32"), "q2": ("sbuf", [128, 32], "int32"), "q3": ("sbuf", [128, 32], "int32"),
-    "q4": ("sbuf", [128, 32], "float32"),
-    "Pr": ("sbuf", [128, 1024], "bfloat16"), "PT": ("sbuf", [128, 1024], "bfloat16"),
-    "xa": ("sbuf", [128, 32], "float32"), "xb": ("sbuf", [128, 32], "float32"), "xc": ("sbuf", [128, 32], "float32"),
-    "xd": ("sbuf", [128, 32], "float32"), "xe": ("sbuf", [128, 32], "float32"), "xf": ("sbuf", [128, 32], "float32"),
-    "FO": ("sbuf", [128, 32], "uint16"),
 }
-SEMAPHORES = ["v", "s", "g", "t", "lw", "lc", "lx", "lv", "ly", "la", "aa", "ab", "out"]
+SEMAPHORES = ["v", "s", "g", "t", "lw", "lc", "lx", "lv", "ly", "la", "a0", "a1", "a2", "out"]
 
 
 def rank_program(g, core, T, topo):
@@ -70,7 +49,10 @@ def rank_program(g, core, T, topo):
 
     V, Sc = g.vector, g.scalar
 
-    for h in range(8):
+    def iota(ap, n, base=0, cm=0, step=1):
+        return done("g", g.iota(ap, [[step, n]], base, cm, allow_small_or_imprecise_dtypes=True))
+
+    for h in range(4):
         q = g.sync if h % 2 == 0 else g.scalar
         q.dma_start(T.Lw[16 * h:16 * h + 16, :], T.want[:, :]).then_inc(S.lw, 16)
     for k in range(4):
@@ -80,9 +62,13 @@ def rank_program(g, core, T, topo):
     g.sync.dma_start(T.wt[:, :], T.w[:, :]).then_inc(S.lv, 16)
 
     kPid = done("g", g.iota(T.pid[:, :], [[1, 1]], 0, 1))
-    kTabG = done("g", g.iota(T.Tab[:, 3104:4096], [[1, 992]], 3104, 0, allow_small_or_imprecise_dtypes=True))
-    kDid = done("g", g.iota(T.did[:, :], [[1, 4]], 4096, 4, allow_small_or_imprecise_dtypes=True))
-    kK16 = done("g", g.iota(T.k16[:, :], [[16, 4]], 0, 1, allow_small_or_imprecise_dtypes=True))
+    kTabG = iota(T.Tab[:, 3104:4096], 992, 3104)
+    kDid = iota(T.did[:, :], 4, 4096, 4)
+    iota(T.Win[:, 2048:2560], 512, step=0)
+    kWin2 = iota(T.Win[:, 6144:6656], 512, step=0)
+    kK16 = iota(T.k16[:, :], 4, 0, 1, 16)
+    iota(T.CW[:, 0:16], 16, step=0)
+    kCz = iota(T.CW[:, 528:544], 16, step=0)
     kOnes = done("v", V.memset(T.ones[:, :], 1.0))
     need("v", kOnes)
     tV0 = done("v", V.tensor_tensor_scan(T.Tab[:, 0:256], T.ones[:, :], T.ones[:, :], -1.0, A.add, A.mult))
@@ -95,43 +81,44 @@ def rank_program(g, core, T, topo):
     kX0 = done("v", V.tensor_scalar(T.xp0[:, :], T.p3[:, :], -127.0, None, A.mult))
     need("v", tV1)
     tV2 = done("v", V.tensor_scalar(T.Tab[:, 512:1024], T.Tab[:, 0:512], 512.0, None, A.add))
-    tV3 = done("v", V.tensor_scalar(T.Tab[:, 1024:1312], T.Tab[:, 0:288], 1024.0, None, A.add))
+    tV3 = done("v", V.tensor_scalar(T.Tab[:, 1024:1504], T.Tab[:, 0:480], 1024.0, None, A.add))
     kWin = done("v", V.memset(T.Win[:, 4096:4608], 0.0))
     need("v", kX0)
     kXp = done("v", V.tensor_scalar(T.xp[:, :], T.pid[:, :], 16.0, T.xp0[:, 0:1], A.mult, A.add))
-    kM = done("v", V.memset(T.M[:, 128:512], 0.0))
     need("v", kXp)
-    kTri = done("v", V.tensor_scalar(T.M[:, 0:128], T.Tab[:, 0:128], T.xp[:, 0:1], BIG, A.is_le, A.mult))
+    kTri = done("v", V.tensor_scalar(T.Win[:, 3968:4096], T.Tab[:, 0:128], T.xp[:, 0:1], BIG, A.is_le, A.mult))
     need("s", tV0)
-    done("s", Sc.activation(T.Tab[:, 1312:1568], T.Tab[:, 0:256], F.Identity, bias=1312.0))
+    done("s", Sc.activation(T.Tab[:, 1504:1760], T.Tab[:, 0:256], F.Identity, bias=1504.0))
     need("s", tV1)
-    done("s", Sc.activation(T.Tab[:, 1568:2080], T.Tab[:, 0:512], F.Identity, bias=1568.0))
+    done("s", Sc.activation(T.Tab[:, 1760:2272], T.Tab[:, 0:512], F.Identity, bias=1760.0))
     need("s", tV2)
-    tS = done("s", Sc.activation(T.Tab[:, 2080:3104], T.Tab[:, 0:1024], F.Identity, bias=2080.0))
+    tS = done("s", Sc.activation(T.Tab[:, 2272:3104], T.Tab[:, 0:832], F.Identity, bias=2272.0))
 
-    need("v", ("lw", 128))
-    kOff0 = done("v", V.tensor_copy(T.off0[:, :], T.Lw[:, :]))
+    need("v", ("lw", 64))
+    done("v", V.tensor_copy(T.off0[0:64, :], T.Lw[0:64, :]))
+    kOff0 = done("v", V.tensor_copy(T.off0[64:128, :], T.Lw[0:64, :]))
     need("v", ("lc", 64))
     kCb = done("v", V.tensor_scalar(T.Cb[:, :], T.C[:, :], BIG, None, A.mult))
     need("v", kOff0, tS, kTabG)
-    kR = done("v", V.tensor_copy(T.R16[:, :], T.Tab[:, 0:4096].indirect(T.off0[:, 0:24])))
+    kR = done("v", V.tensor_copy(T.R16[:, :], T.Tab[:, 0:4096].indirect(T.off0[:, 0:20])))
     kC = done("v", V.tensor_copy(T.Cf[:, :], T.C[:, :]))
     need("s", kOff0, tV3, tS, kTabG)
-    kRS = done("s", Sc.activation(T.RS[:, :], T.Tab[:, 0:4096].indirect(T.off0[:, 24:32]), F.Copy))
+    kRS = done("s", Sc.activation(T.RS[:, :], T.Tab[:, 0:4096].indirect(T.off0[:, 20:32]), F.Copy))
     E = [T.E0, T.E1, T.E2, T.E3]
     need("s", kRS, kCb)
-    kS = [done("s", Sc.activation(E[k][:, 384 - 128 * k:512 - 128 * k], T.RS[:, :], F.Abs, bias=T.Cb[:, k:k + 1], scale=-BIG)) for k in range(4)]
+    kS, kE = {}, {}
+    for k in (3, 2, 1, 0):
+        lo = max(128 * k, 320)
+        kS[k] = done("s", Sc.activation(E[k][:, lo - 128 * k:512 - 128 * k], T.RS[:, lo - 320:192], F.Abs, bias=T.Cb[:, k:k + 1], scale=-BIG))
     need("v", kR, kC)
-    kE = [done("v", V.tensor_scalar(E[k][:, 0:384 - 128 * k], T.R16[:, 128 * k:384], T.Cf[:, k:k + 1], BIG, A.not_equal, A.mult)) for k in range(3)]
-    need("v", kTri, kM)
-    for k in range(4):
+    for k in (2, 1, 0):
+        kE[k] = done("v", V.tensor_scalar(E[k][:, 0:320 - 128 * k], T.R16[:, 128 * k:320], T.Cf[:, k:k + 1], BIG, A.not_equal, A.mult))
+    need("v", kTri, kWin)
+    for k in (3, 2, 1, 0):
         need("v", kS[k])
         if k < 3:
             need("v", kE[k])
-        kN = done("v", V.tensor_tensor_scan(T.NB[:, 640 * k:512 * k + 512], E[k][:, :], T.M[:, 0:512 - 128 * k], BIG, A.min, A.max))
-    need("s", kWin)
-    done("s", Sc.activation(T.Win[:, 2048:2560], T.Win[:, 4096:4608], F.Copy))
-    kWin2 = done("s", Sc.activation(T.Win[:, 6144:6656], T.Win[:, 4096:4608], F.Copy))
+        kN = done("v", V.tensor_tensor_scan(T.NB[:, 640 * k:512 * k + 512], E[k][:, :], T.Win[:, 3968:4480 - 128 * k], BIG, A.min, A.max))
     need("v", kN, kDid)
     kK = done("v", V.tensor_tensor(T.K[:, :], T.did[:, :], T.NB[:, 511:2048:512], A.subtract))
     need("v", kK)
@@ -157,14 +144,14 @@ def rank_program(g, core, T, topo):
     need("v", kTG, kGsh)
     done("v", V.tensor_scalar(T.off1[0:64, :], T.TG[0:64, 0:16], T.gsh[0:64, 0:1], None, A.add))
     kO1 = done("v", V.tensor_scalar(T.off1[64:128, :], T.TG[64:128, 16:32], T.gsh[64:128, 0:1], None, A.add))
-    need("v", kT2, kK16)
-    kThr = done("v", V.tensor_scalar(T.thr[:, :], T.k16[:, :], T.t2[:, 0:1], None, A.add))
     need("v", kO1, kWin, kWin2)
     kSc = done("v", V.tensor_copy(T.Win[:, 0:8704].indirect(T.off1[:, 0:16]), T.ones[:, :]))
     need("v", kSc)
     need("s", kSc)
     done("v", V.tensor_copy(T.OB[0:64, :], T.Win[64:128, 2048:2560]))
     o1 = done("v", V.tensor_copy(T.OB[64:128, 0:160], T.Win[0:64, 6144:6304]))
+    need("v", kT2, kK16)
+    kThr = done("v", V.tensor_scalar(T.thr[:, :], T.k16[:, :], T.t2[:, 0:1], None, A.add))
     o2 = done("s", Sc.activation(T.OB[64:128, 160:512], T.Win[0:64, 6304:6656], F.Copy))
     need("v", o1, o2)
     kCum = done("v", V.tensor_tensor_scan(T.CW[:, 16:528], T.Win[:, 4096:4608], T.OB[:, :], 0.0, A.add, A.add))
@@ -178,55 +165,55 @@ def rank_program(g, core, T, topo):
     c2 = done("v", V.tensor_reduce(T.LR[:, 30:31], T.J2[:, :], AxisListType.X, A.add))
     sent = [0]
 
+    def mask(dst, pick):
+        es = topo.engines(core, dst)
+        m = 0
+        for j in pick(len(es)):
+            m |= 1 << es[j]
+            sent[0] += 1
+        return m
+
+    def at(dst):
+        rid, pid, _ = topo.addr(dst)
+        return DstId(rid=rid, pnc=pid)
+
     def fused(items):
         tr = []
-        for dst, src, out, sem, eng in items:
-            dc = T.cores[dst]
-            rid, pid, _ = topo.addr(dc)
-            es = topo.engines(core, dc)
-            m = 0
-            for j in eng(len(es)):
-                m |= 1 << es[j]
-                sent[0] += 1
-            tr.append(RemoteDMATransfer(dst_ids=[DstId(rid=rid, pnc=pid)], dma_engine_mask=m, remote_sem=sem, src=src, dst=out))
+        for d, src, out, sem, pick in items:
+            c = T.cores[d]
+            tr.append(RemoteDMATransfer(dst_ids=[at(c)], dma_engine_mask=mask(c, pick), remote_sem=sem, src=src, dst=out))
         g.remote_dma_fused(tr, local_sem=S.out)
 
     def every(i, n):
         return lambda ne: range(i, ne, n)
 
     need("g", c1, z3, c2)
-    fused([((r - 1 - i) % N, T.LR[:, 28:32], T.LR[:, 4 * i:4 * i + 4], S.la, every(i, 8)) for i in range(7)])
+    to = [T.cores[(r - 1 - i) % N] for i in range(7)]
+    g.remote_dma_fused([RemoteDMATransfer(dst_ids=[at(c) for c in to], dma_engine_mask=mask(to[0], every(0, 1)), remote_sem=S.la,
+                                          srcs=[T.LR[:, 28:32]], dsts=[T.LR[:, 4 * i:4 * i + 4] for i in range(7)])], local_sem=S.out)
+    nla = 7 * sent[0]
 
-    need("v", ("lx", 16))
-    for t in (0, 1):
-        kPlV = done("v", V.tensor_copy(T.XP[:, PL * t:PL * t + 512], T.x0[:, t:2048:4]))
-    for t in range(4):
-        kPad = done("v", V.memset(T.XP[:, PL * t + 512:PL * t + 528], 0.0))
-    need("s", ("lx", 16))
-    for t in (2, 3):
-        kPlS = done("s", Sc.activation(T.XP[:, PL * t:PL * t + 512], T.x0[:, t:2048:4], F.Copy))
-    kGsh2 = done("v", V.tensor_scalar(T.gsh2[:, :], T.p4[:, :], -512.0, 16.0, A.mult, A.add))
-    need("v", ("lv", 16))
-    kW = done("v", V.quantize_mx(T.QW[:, :], T.SW[:, :], T.wt[:, :]))
-    need("v", kGsh2)
-    ko1 = done("v", V.tensor_scalar(T.o1[:, :], T.Lw[:, :], T.gsh2[:, 0:1], 528.0, A.add, A.min))
-    kq1 = done("v", V.tensor_scalar(T.q1[:, :], T.Lw[:, :], 9, None, A.arith_shift_right))
-    done("v", V.memset(T.CW[:, 0:16], 0.0))
-    kCz = done("v", V.memset(T.CW[:, 528:544], 0.0))
+    need("v", kGsh)
+    ko1 = done("v", V.tensor_scalar(T.o1[:, :], T.off0[:, :], T.gsh[:, 0:1], 4608.0, A.add, A.min))
+    kq0 = done("v", V.tensor_copy(T.q0[:, :], T.off0[:, :]))
     need("v", ko1)
-    done("v", V.tensor_scalar(T.OP[:, 0:64:2], T.o1[:, :], 15.0, None, A.max))
-    kOP = done("v", V.tensor_scalar(T.OP[:, 1:64:2], T.o1[:, :], 15.0, None, A.max))
-    need("v", kq1)
-    kq2 = done("v", V.tensor_scalar(T.q2[:, :], T.q1[:, :], -1.0, float(r + 7), A.mult, A.add))
-    need("v", kq2)
-    kq3 = done("v", V.tensor_scalar(T.q3[:, :], T.q2[:, :], 7, None, A.bitwise_and))
-    need("v", kq3)
-    kq4 = done("v", V.tensor_scalar(T.q4[:, :], T.q3[:, :], 48.0, -1.0, A.mult, A.add))
+    done("v", V.tensor_scalar(T.OP[:, 0:64:2], T.o1[:, :], 4095.0, -4080.0, A.max, A.add))
+    kOP = done("v", V.tensor_scalar(T.OP[:, 1:64:2], T.o1[:, :], 4095.0, -4080.0, A.max, A.add))
+    need("v", ("lx", 16))
+    for t in (0, 1, 2):
+        done("v", V.tensor_copy(T.XP[:, PL * t:PL * t + 512], T.x0[:, t:2048:4]))
+    kPad = done("v", V.memset(T.XP[:, 512:4 * PL:PL], 0.0))
+    need("s", ("lx", 16))
+    kPlS = done("s", Sc.activation(T.XP[:, PL * 3:PL * 3 + 512], T.x0[:, 3:2048:4], F.Copy))
+    need("s", kOP, kCz, kCum)
+    kPs = done("s", Sc.activation(T.Pr[:, 384:1024], T.CW[:, 0:544].indirect(T.OP[:, 24:64]), F.Copy))
+    need("v", kOP, kCz, kCum)
+    kPv = done("v", V.tensor_copy(T.Pr[:, 0:384], T.CW[:, 0:544].indirect(T.OP[:, 0:24])))
 
     a, b = divmod(r, 2)
     ra = slice(32 * a, 32 * a + 32)
     hb = slice(16 * b, 16 * b + 16)
-    need("v", ("la", 14), c1, c2)
+    need("v", ("la", nla), c1, c2)
     kX1 = done("v", V.transpose(T.X1[ra, :], T.LR[ra, :]))
     need("v", kX1)
     need("s", kX1)
@@ -234,89 +221,108 @@ def rank_program(g, core, T, topo):
     kcs = kcv = None
     for n, (d, u) in enumerate(todo):
         o = T.X1[32 * d:32 * d + 32, 16 * u:16 * u + 16]
-        if n < 3:
+        if n < 2:
             kcs = done("s", Sc.activation(o, T.X1[ra, hb], F.Copy))
         else:
             kcv = done("v", V.tensor_copy(o, T.X1[ra, hb]))
     need("v", kcs, kcv)
     kX3 = done("v", V.transpose(T.X3[:, :], T.X1[:, :]))
     need("v", kX3)
-    done("v", V.tensor_scalar(T.O[:, 0:24:3], T.X3[:, 0:32:4], 0.5, 256.0, A.mult, A.add))
-    done("v", V.tensor_scalar(T.O[:, 1:24:3], T.X3[:, 1:32:4], 0.5, 256.0, A.mult, A.add))
-    kO = done("v", V.tensor_copy(T.O[:, 2:24:3], T.X3[:, 2:32:4]))
+    done("v", V.tensor_scalar(T.O[:, 0:21:3], T.X3[:, 0:28:4], 0.5, 256.0, A.mult, A.add))
+    done("v", V.tensor_scalar(T.O[:, 1:21:3], T.X3[:, 1:28:4], 0.5, 256.0, A.mult, A.add))
+    kO = done("v", V.tensor_copy(T.O[:, 2:21:3], T.X3[:, 2:28:4]))
+
+    def pick(h, o, t, lo, hi):
+        return h[:, 64 * lo + t:64 * hi:4], T.XP[:, PL * t:PL * t + 513].indirect(o[:, lo:hi])
+
+    part = [(0, 8), (8, 16), (16, 21)]
     need("s", kO, kPlS, kPad)
-    kh = {}
-    for nm, H, c in (("A", T.HA, 0), ("B", T.HB, 12)):
+    kh = []
+    for lo, hi in part:
         for t in (2, 3):
-            kh[nm] = done("s", Sc.activation(H[:, t:768:4], T.XP[:, PL * t:PL * t + 513].indirect(T.O[:, c:c + 12]), F.Copy))
-    need("v", kO, kPlV, kPad)
-    kq = {}
-    for nm, H, c, Q, P in (("A", T.HA, 0, T.QA, T.SA), ("B", T.HB, 12, T.QB, T.SB)):
-        for t in (0, 1):
-            kv = done("v", V.tensor_copy(H[:, t:768:4], T.XP[:, PL * t:PL * t + 513].indirect(T.O[:, c:c + 12])))
-        need("v", kv, kh[nm])
-        kq[nm] = done("v", V.quantize_mx(Q[:, :], P[:, :], H[:, :]))
+            k = done("s", Sc.activation(*pick(T.H, T.O, t, lo, hi), F.Copy))
+        kh.append(k)
+    need("v", kO, kPlS, kPad)
+    eng = {2: [every(0, 2), every(1, 2)], 3: [every(0, 2), every(1, 4), every(3, 4)]}
+    flip = {2: [every(1, 2), every(0, 2)], 3: [every(1, 2), every(0, 4), every(2, 4)]}
+    kv = {}
+    for n, ids in enumerate(((0, 1), (2, 3, 4), (5, 6))):
+        for m, t in ((n, 0), (n, 1), (n + 1, 0)):
+            if m < 3 and (m, t) not in kv:
+                kv[m, t] = done("v", V.tensor_copy(*pick(T.H, T.O, t, *part[m])))
+        q, p, lo, c0 = (T.Q, T.SQ, 128 * n, 0) if n < 2 else (T.Q2, T.S2, 0, 208)
+        need("v", kv[n, 0], kv[n, 1], kh[n])
+        kq = done("v", V.quantize_mx(q[:, lo:lo + 128], p[:, lo:lo + 128], T.H[:, 4 * (lo + c0):4 * (lo + c0) + 512]))
+        need("g", kq)
+        to = [((r + 1 + i) % N, slice(CAP * i - c0, CAP * i - c0 + CAP), slice(CAP * i, CAP * i + CAP)) for i in ids]
+        sem = S["a%d" % n]
+        fused([(d, q[:, c].bitcast(dt.uint8), T.CR[:, e].bitcast(dt.uint8), sem, m) for (d, c, e), m in zip(to, eng[len(to)])])
+        fused([(d, p[:, c], T.SR[:, e], sem, m) for (d, c, e), m in zip(to, flip[len(to)])])
+    done("v", V.tensor_scalar(T.OO[:, 0:2], T.X3[:, 28:30], 0.5, 256.0, A.mult, A.add))
+    kOO = done("v", V.tensor_copy(T.OO[:, 2:3], T.X3[:, 30:31]))
+    need("s", kOO)
+    for t in range(4):
+        kHo = done("s", Sc.activation(*pick(T.HO, T.OO, t, 0, 3), F.Copy))
+    need("v", ("lv", 16))
+    kW = done("v", V.quantize_mx(T.QW[:, :], T.SW[:, :], T.wt[:, :]))
 
-    def codes(q, lo):
-        return q[:, lo:lo + CAP].bitcast(dt.uint8)
-
-    need("g", kq["A"])
-    fused([((r + 1 + i) % N, codes(T.QA, 48 * i), codes(T.CR, 48 * i), S.aa, every(i, 4)) for i in range(4)])
-    fused([((r + 1 + i) % N, T.SA[:, 48 * i:48 * i + 48], T.SR[:, 48 * i:48 * i + 48], S.aa, every(i, 4)) for i in range(4)])
-    need("g", kq["B"])
-    half = [every(0, 2), every(1, 4), every(3, 4)]
-    flip = [every(1, 2), every(0, 4), every(2, 4)]
-    fused([((r + 5 + i) % N, codes(T.QB, 48 * i), codes(T.CR, 192 + 48 * i), S.ab, half[i]) for i in range(3)])
-    fused([((r + 5 + i) % N, T.SB[:, 48 * i:48 * i + 48], T.SR[:, 192 + 48 * i:240 + 48 * i], S.ab, flip[i]) for i in range(3)])
-
-    ts = g.tensor
-    need("t", kW, kq["B"])
-    m0 = done("t", ts.matmul_mx(T.po[:, 0:128], T.QW[:, :], T.SW[:, :], T.QB[:, 64:192], T.SB[:, 64:192], True, True))
-    need("t", ("aa", 32))
-    m1 = done("t", ts.matmul_mx(T.pa[:, 0:192], T.QW[:, :], T.SW[:, :], T.CR[:, 0:192], T.SR[:, 0:192], True, True))
-    need("t", ("ab", 32))
-    m2 = done("t", ts.matmul_mx(T.pb[:, 0:144], T.QW[:, :], T.SW[:, :], T.CR[:, 192:336], T.SR[:, 192:336], True, True))
-
-    need("s", kOP, kCz, kCum)
-    kPs = done("s", Sc.activation(T.Pr[:, 512:1024], T.CW[:, 0:544].indirect(T.OP[:, 32:64]), F.Copy))
-    need("v", kOP, kCz, kCum)
-    kPv = done("v", V.tensor_copy(T.Pr[:, 0:512], T.CW[:, 0:544].indirect(T.OP[:, 0:32])))
     need("v", kPs, kPv)
     kPT = done("v", V.transpose(T.PT[:, :], T.Pr[:, :]))
+    kHz = done("v", V.memset(T.HO[:, 192:512], 0.0))
+    need("v", kq0)
+    kq1 = done("v", V.tensor_scalar(T.q1[:, :], T.q0[:, :], 9, None, A.arith_shift_right))
     need("v", kPT)
     kxa = done("v", V.tensor_tensor(T.xa[:, :], T.PT[:, 0:1024:32], T.PT[:, 16:1024:32], A.add))
     need("v", kxa)
     need("s", kxa)
     x1 = done("v", V.tensor_copy(T.xb[0:64, :], T.xa[64:128, :]))
     x2 = done("s", Sc.activation(T.xb[64:128, :], T.xa[0:64, :], F.Copy))
+    need("v", kq1)
+    kq2 = done("v", V.tensor_scalar(T.q2[:, :], T.q1[:, :], -1.0, float(r + 7), A.mult, A.add))
+    need("v", kHo, kHz)
+    kqo = done("v", V.quantize_mx(T.QO[:, :], T.SO[:, :], T.HO[:, :]))
     need("v", x1, x2)
     kxc = done("v", V.tensor_tensor(T.xc[:, :], T.xa[:, :], T.xb[:, :], A.add))
-    need("v", kxc, kq4)
+    need("v", kq2)
+    kq3 = done("v", V.tensor_scalar(T.q3[:, :], T.q2[:, :], 7, None, A.bitwise_and))
+    need("v", kxc)
     need("s", kxc)
     done("v", V.tensor_copy(T.xd[0:32, :], T.xc[32:64, :]))
     x3 = done("v", V.tensor_copy(T.xd[32:64, :], T.xc[0:32, :]))
     done("s", Sc.activation(T.xd[64:96, :], T.xc[96:128, :], F.Copy))
     x4 = done("s", Sc.activation(T.xd[96:128, :], T.xc[64:96, :], F.Copy))
+    need("v", kq3)
+    kq4 = done("v", V.tensor_scalar(T.q4[:, :], T.q3[:, :], 48.0, -1.0, A.mult, A.add))
+    need("v", kq4)
     kxe = done("v", V.tensor_tensor(T.xe[:, :], T.xc[:, :], T.q4[:, :], A.add))
     need("v", x3, x4, kxe)
     kxf = done("v", V.tensor_tensor(T.xf[:, :], T.xe[:, :], T.xd[:, :], A.add))
     need("v", kxf)
     kFO = done("v", V.tensor_copy(T.FO[:, :], T.xf[:, :]))
 
+    ts = g.tensor
+    need("t", kW, kqo)
+    m0 = done("t", ts.matmul_mx(T.po[:, 0:128], T.QW[:, :], T.SW[:, :], T.QO[:, :], T.SO[:, :], True, True))
+    need("t", ("a0", 32), ("a1", 32))
+    m1 = done("t", ts.matmul_mx(T.pa[:, 0:240], T.QW[:, :], T.SW[:, :], T.CR[:, 0:240], T.SR[:, 0:240], True, True))
+    need("t", ("a2", 32))
+    m2 = done("t", ts.matmul_mx(T.pb[:, 0:128], T.QW[:, :], T.SW[:, :], T.CR[:, 208:336], T.SR[:, 208:336], True, True))
+
     need("v", m0)
-    zo = done("v", V.tensor_copy(T.Z[:, 336:384], T.po[:, 80:128]))
+    zo = done("v", V.tensor_copy(T.Z[:, 336:384], T.po[:, 0:48]))
     need("s", m1)
-    za = done("s", Sc.activation(T.Z[:, 0:192], T.pa[:, 0:192], F.Copy))
+    za = done("s", Sc.activation(T.Z[:, 0:240], T.pa[:, 0:240], F.Copy))
     need("v", m2)
-    zb = done("v", V.tensor_copy(T.Z[:, 192:336], T.pb[:, 0:144]))
+    zb = done("v", V.tensor_copy(T.Z[:, 240:336], T.pb[:, 32:128]))
     need("v", kFO, zo, za, zb)
-    yv = done("v", V.tensor_copy(T.yv[:, :], T.Z[:, 0:384].indirect(T.FO[:, 0:16])))
     need("s", kFO, zo, za, zb)
-    ysc = done("s", Sc.activation(T.ys[:, :], T.Z[:, 0:384].indirect(T.FO[:, 16:32]), F.Copy))
-    need("y", yv)
-    g.sync.dma_start(T.y[:, 0:256], T.yv[:, :]).then_inc(S.ly, 16)
-    need("s", ysc)
-    g.scalar.dma_start(T.y[:, 256:512], T.ys[:, :]).then_inc(S.ly, 16)
+    for lo, hi, qn in ((0, 6, "y"), (6, 16, "s")):
+        ky = done("v", V.tensor_copy(T.yv[:, 16 * lo:16 * hi], T.Z[:, 0:384].indirect(T.FO[:, lo:hi])))
+        need("y", ky)
+        g.sync.dma_start(T.y[:, 16 * lo:16 * hi], T.yv[:, 16 * lo:16 * hi]).then_inc(S.ly, 16)
+        ky = done("s", Sc.activation(T.ys[:, 16 * lo:16 * hi], T.Z[:, 0:384].indirect(T.FO[:, 16 + lo:16 + hi]), F.Copy))
+        need(qn, ky)
+        queues[qn].dma_start(T.y[:, 256 + 16 * lo:256 + 16 * hi], T.ys[:, 16 * lo:16 * hi]).then_inc(S.ly, 16)
 
     need("g", ("out", sent[0]), ("v", cnt["v"]), ("s", cnt["s"]), ("g", cnt["g"]), ("t", cnt["t"]))
-    need("g", ("lw", 128), ("lc", 64), ("lx", 16), ("lv", 16), ("ly", 32), ("la", 14), ("aa", 32), ("ab", 32))
+    need("g", ("lw", 64), ("lc", 64), ("lx", 16), ("lv", 16), ("ly", 64), ("la", nla), ("a0", 32), ("a1", 32), ("a2", 32))

@@ -13,17 +13,17 @@ def sb(kind, **widths):
 
 
 SCRATCH = {
-    **sb("int32", Lw=32, C=4, pid=1, p4=1, p3=1, q0=32, q1=32, q2=32, q3=32),
-    **sb("uint16", off0=32, R16=320, off1=16, O=24, OO=4, OP=64, FO=32),
-    **sb("float32", Cf=4, Cb=4, Tab=4096, RS=192, xp0=1, xp=1, t2=1, gsh=1, did=4, k16=4, thr=4, K=4, G=40, TG=32,
+    **sb("int32", Lw=32, D=16, Ei=32, pid=1, p4=1, q0=32, q1=32, q2=32, q3=32),
+    **sb("uint16", off0=32, EO=32, off1=16, O=24, OO=4, OP=64, FO=32),
+    **sb("float32", Cf=4, Cb=4, Dc=16, X=512, R=512, row=128, bt=1, p4f=1, t2=1, gsh=1, did=4, k16=4, thr=4, K=4, G=40, TG=32,
          J0=512, J1=512, LR=32, X1=32, X3=32, Z=384, yv=256, ys=256, o1=32, q4=32, xa=32, xb=32, xc=32, xd=32, xe=32, xf=32),
-    **sb("bfloat16", E0=512, E1=384, E2=256, E3=128, NB=2048, ones=256, Win=8704, OB=512, CW=544, J2=512,
+    **sb("bfloat16", E0=512, E1=384, E2=256, E3=128, NB=2048, MK=640, ones=256, Win=8704, OB=512, CW=544, J2=512,
          x0=2048, XP=4 * PL, wt=512, H=1344, HO=512, Pr=1024, PT=1024),
     **sb("float8_e4m3fn_x4", Q=256, Q2=128, QO=128, QW=128, CR=336),
     **sb("uint8", SQ=256, S2=128, SO=128, SW=128, SR=336),
     "pa": ("psum", [128, 512], "float32"), "pb": ("psum", [128, 512], "float32"), "po": ("psum", [128, 512], "float32"),
 }
-SEMAPHORES = ["v", "s", "g", "t", "lw", "lc", "lx", "lv", "ly", "la", "a0", "a1", "a2", "out"]
+SEMAPHORES = ["v", "s", "g", "t", "ld", "lz", "lw", "lx", "lv", "ly", "la", "a0", "a1", "a2", "out"]
 
 
 def rank_program(g, core, T, topo):
@@ -52,74 +52,70 @@ def rank_program(g, core, T, topo):
     def iota(ap, n, base=0, cm=0, step=1):
         return done("g", g.iota(ap, [[step, n]], base, cm, allow_small_or_imprecise_dtypes=True))
 
+    for e in range(4):
+        q = g.sync if e % 2 == 0 else g.scalar
+        q.dma_start(T.D[32 * e:32 * e + 32, :], T.want[:, :]).then_inc(S.ld, 16)
+
+    kEi = done("g", g.iota(T.Ei[:, :], [[1, 16], [0, 2]], 0, 0))
+    kPid = done("g", g.iota(T.pid[:, :], [[1, 1]], 0, 1))
+    kBt = iota(T.bt[:, :], 1, int(BIG), int(BIG))
+    kRow = iota(T.row[:, :], 128)
+    kK16 = iota(T.k16[:, :], 4, 0, 1, 16)
+    kDid = iota(T.did[:, :], 4, 4096, 4)
+    kOnes = iota(T.ones[:, :], 256, 1, step=0)
+    kWin2 = iota(T.Win[:, 6144:6656], 512, step=0)
+    iota(T.CW[:, 0:16], 16, step=0)
+    kCz = iota(T.CW[:, 528:544], 16, step=0)
+    kMz = done("v", V.memset(T.MK[:, 128:640], 0.0))
+    need("v", kEi)
+    kEO = done("v", V.tensor_copy(T.EO[:, :], T.Ei[:, :]))
+    need("v", kPid)
+    kP4 = done("v", V.tensor_scalar(T.p4[:, :], T.pid[:, :], 4, None, A.arith_shift_right))
+    need("v", kP4)
+    kP4f = done("v", V.tensor_copy(T.p4f[:, :], T.p4[:, :]))
+    z3 = done("v", V.memset(T.LR[:, 31:32], 0.0))
+    need("y", kMz)
+    for lo in (4096, 2048):
+        g.sync.dma_start(T.Win[:, lo:lo + 512], T.MK[:, 128:640]).then_inc(S.lz, 16)
     for h in range(4):
-        q = g.sync if h % 2 == 0 else g.scalar
-        q.dma_start(T.Lw[16 * h:16 * h + 16, :], T.want[:, :]).then_inc(S.lw, 16)
-    for k in range(4):
-        q = g.sync if k % 2 == 0 else g.scalar
-        q.dma_start(T.C[:, k:k + 1], T.want[:, 8 * k:8 * k + 8]).then_inc(S.lc, 16)
+        g.sync.dma_start(T.Lw[16 * h:16 * h + 16, :], T.want[:, :]).then_inc(S.lw, 16)
     g.sync.dma_start(T.x0[:, :], T.x[:, :]).then_inc(S.lx, 16)
     g.sync.dma_start(T.wt[:, :], T.w[:, :]).then_inc(S.lv, 16)
 
-    kPid = done("g", g.iota(T.pid[:, :], [[1, 1]], 0, 1))
-    kTabG = iota(T.Tab[:, 3104:4096], 992, 3104)
-    kDid = iota(T.did[:, :], 4, 4096, 4)
-    iota(T.Win[:, 2048:2560], 512, step=0)
-    kWin2 = iota(T.Win[:, 6144:6656], 512, step=0)
-    kK16 = iota(T.k16[:, :], 4, 0, 1, 16)
-    iota(T.CW[:, 0:16], 16, step=0)
-    kCz = iota(T.CW[:, 528:544], 16, step=0)
-    kOnes = done("v", V.memset(T.ones[:, :], 1.0))
-    need("v", kOnes)
-    tV0 = done("v", V.tensor_tensor_scan(T.Tab[:, 0:256], T.ones[:, :], T.ones[:, :], -1.0, A.add, A.mult))
-    need("v", kPid)
-    kP4 = done("v", V.tensor_scalar(T.p4[:, :], T.pid[:, :], 4, None, A.arith_shift_right))
-    kP3 = done("v", V.tensor_scalar(T.p3[:, :], T.pid[:, :], 3, None, A.arith_shift_right))
-    need("v", tV0)
-    tV1 = done("v", V.tensor_scalar(T.Tab[:, 256:512], T.Tab[:, 0:256], 256.0, None, A.add))
-    need("v", kP3)
-    kX0 = done("v", V.tensor_scalar(T.xp0[:, :], T.p3[:, :], -127.0, None, A.mult))
-    need("v", tV1)
-    tV2 = done("v", V.tensor_scalar(T.Tab[:, 512:1024], T.Tab[:, 0:512], 512.0, None, A.add))
-    tV3 = done("v", V.tensor_scalar(T.Tab[:, 1024:1504], T.Tab[:, 0:480], 1024.0, None, A.add))
-    kWin = done("v", V.memset(T.Win[:, 4096:4608], 0.0))
-    need("v", kX0)
-    kXp = done("v", V.tensor_scalar(T.xp[:, :], T.pid[:, :], 16.0, T.xp0[:, 0:1], A.mult, A.add))
-    need("v", kXp)
-    kTri = done("v", V.tensor_scalar(T.Win[:, 3968:4096], T.Tab[:, 0:128], T.xp[:, 0:1], BIG, A.is_le, A.mult))
-    need("s", tV0)
-    done("s", Sc.activation(T.Tab[:, 1504:1760], T.Tab[:, 0:256], F.Identity, bias=1504.0))
-    need("s", tV1)
-    done("s", Sc.activation(T.Tab[:, 1760:2272], T.Tab[:, 0:512], F.Identity, bias=1760.0))
-    need("s", tV2)
-    tS = done("s", Sc.activation(T.Tab[:, 2272:3104], T.Tab[:, 0:832], F.Identity, bias=2272.0))
-
-    need("v", ("lw", 64))
-    done("v", V.tensor_copy(T.off0[0:64, :], T.Lw[0:64, :]))
-    kOff0 = done("v", V.tensor_copy(T.off0[64:128, :], T.Lw[0:64, :]))
-    need("v", ("lc", 64))
-    kCb = done("v", V.tensor_scalar(T.Cb[:, :], T.C[:, :], BIG, None, A.mult))
-    need("v", kOff0, tS, kTabG)
-    kR = done("v", V.tensor_copy(T.R16[:, :], T.Tab[:, 0:4096].indirect(T.off0[:, 0:20])))
-    kC = done("v", V.tensor_copy(T.Cf[:, :], T.C[:, :]))
-    need("s", kOff0, tV3, tS, kTabG)
-    kRS = done("s", Sc.activation(T.RS[:, :], T.Tab[:, 0:4096].indirect(T.off0[:, 20:32]), F.Copy))
+    need("v", ("ld", 64))
+    kDc = done("v", V.tensor_scalar(T.Dc[:, :], T.D[:, :], BIG, None, A.mult))
+    need("v", kEO)
+    kXv = done("v", V.tensor_scalar(T.X[:, 0:320], T.D[:, 0:16].indirect(T.EO[:, 0:20]), BIG, None, A.mult))
+    need("s", kDc, kEO)
+    kXs = done("s", Sc.activation(T.X[:, 320:512], T.Dc[:, 0:16].indirect(T.EO[:, 20:32]), F.Copy))
+    need("s", kBt, kRow)
+    kTri = done("s", Sc.activation(T.MK[:, 0:128], T.row[:, :], F.Relu, bias=T.bt[:, 0:1], scale=-BIG))
+    for e in range(4):
+        h = slice(32 * e, 32 * e + 32)
+        kCb = done("s", Sc.activation(T.Cb[h, :], T.Dc[h, e:16:4], F.Copy))
+    need("v", kXv, kXs)
+    kR1 = done("v", V.transpose(T.R[:, 256:512], T.X[:, 256:512]))
+    kR0 = done("v", V.transpose(T.R[:, 0:256], T.X[:, 0:256]))
     E = [T.E0, T.E1, T.E2, T.E3]
-    need("s", kRS, kCb)
+    need("s", kR1, kCb)
     kS, kE = {}, {}
     for k in (3, 2, 1, 0):
-        lo = max(128 * k, 320)
-        kS[k] = done("s", Sc.activation(E[k][:, lo - 128 * k:512 - 128 * k], T.RS[:, lo - 320:192], F.Abs, bias=T.Cb[:, k:k + 1], scale=-BIG))
-    need("v", kR, kC)
-    for k in (2, 1, 0):
-        kE[k] = done("v", V.tensor_scalar(E[k][:, 0:320 - 128 * k], T.R16[:, 128 * k:320], T.Cf[:, k:k + 1], BIG, A.not_equal, A.mult))
-    need("v", kTri, kWin)
+        lo = max(128 * k, 256)
+        kS[k] = done("s", Sc.activation(E[k][:, lo - 128 * k:512 - 128 * k], T.R[:, lo:512], F.Abs, bias=T.Cb[:, k:k + 1], scale=-1.0))
+    kC = done("s", Sc.activation(T.Cf[:, :], T.Cb[:, :], F.Copy, scale=1.0 / BIG))
+    need("s", kP4f)
+    kGsh = done("s", Sc.activation(T.gsh[:, :], T.p4f[:, :], F.Identity, bias=4096.0, scale=-512.0))
+    kT2 = done("s", Sc.activation(T.t2[:, :], T.p4f[:, :], F.Identity, bias=0.5, scale=-16.0))
+    need("v", kR0, kCb)
+    for k in (1, 0):
+        kE[k] = done("v", V.tensor_scalar(E[k][:, 0:256 - 128 * k], T.R[:, 128 * k:256], T.Cb[:, k:k + 1], BIG, A.not_equal, A.mult))
+    need("v", kTri, kMz)
     for k in (3, 2, 1, 0):
         need("v", kS[k])
-        if k < 3:
+        if k < 2:
             need("v", kE[k])
-        kN = done("v", V.tensor_tensor_scan(T.NB[:, 640 * k:512 * k + 512], E[k][:, :], T.Win[:, 3968:4480 - 128 * k], BIG, A.min, A.max))
-    need("v", kN, kDid)
+        kN = done("v", V.tensor_tensor_scan(T.NB[:, 640 * k:512 * k + 512], E[k][:, :], T.MK[:, 0:512 - 128 * k], BIG, A.min, A.max))
+    need("v", kN, kDid, kC)
     kK = done("v", V.tensor_tensor(T.K[:, :], T.did[:, :], T.NB[:, 511:2048:512], A.subtract))
     need("v", kK)
     e1 = done("v", V.tensor_tensor(T.G[:, 0:4], T.K[:, :], T.Cf[:, :], A.max))
@@ -130,28 +126,26 @@ def rank_program(g, core, T, topo):
     a1 = done("v", V.tensor_copy(T.G[0:64, 8:12], T.G[64:128, 0:4]))
     done("s", Sc.activation(T.G[64:128, 4:8], T.G[0:64, 0:4], F.Copy))
     b1 = done("s", Sc.activation(T.G[64:128, 8:12], T.G[0:64, 0:4], F.Copy))
-    kGsh = done("v", V.tensor_scalar(T.gsh[:, :], T.p4[:, :], -512.0, 4096.0, A.mult, A.add))
     need("v", a1, b1, e2)
-    need("s", a1, b1)
+    need("s", a1, b1, e2)
     done("v", V.tensor_copy(T.G[0:32, 16:32], T.G[32:64, 0:16]))
     done("v", V.tensor_copy(T.G[32:64, 16:32], T.G[0:32, 0:16]))
     a2 = done("v", V.tensor_copy(T.G[:, 32:40], T.G[:, 0:8]))
     done("s", Sc.activation(T.G[64:96, 16:32], T.G[96:128, 0:16], F.Copy))
     b2 = done("s", Sc.activation(T.G[96:128, 16:32], T.G[64:96, 0:16], F.Copy))
-    kT2 = done("v", V.tensor_scalar(T.t2[:, :], T.p4[:, :], -16.0, 0.5, A.mult, A.add))
+    need("s", kT2, kK16)
+    kThr = done("s", Sc.activation(T.thr[:, :], T.k16[:, :], F.Identity, bias=T.t2[:, 0:1]))
     need("v", a2, b2)
     kTG = done("v", V.transpose(T.TG[:, :], T.G[:, 8:40]))
     need("v", kTG, kGsh)
     done("v", V.tensor_scalar(T.off1[0:64, :], T.TG[0:64, 0:16], T.gsh[0:64, 0:1], None, A.add))
     kO1 = done("v", V.tensor_scalar(T.off1[64:128, :], T.TG[64:128, 16:32], T.gsh[64:128, 0:1], None, A.add))
-    need("v", kO1, kWin, kWin2)
+    need("v", kO1, kOnes, kWin2, ("lz", 32))
     kSc = done("v", V.tensor_copy(T.Win[:, 0:8704].indirect(T.off1[:, 0:16]), T.ones[:, :]))
     need("v", kSc)
     need("s", kSc)
     done("v", V.tensor_copy(T.OB[0:64, :], T.Win[64:128, 2048:2560]))
     o1 = done("v", V.tensor_copy(T.OB[64:128, 0:160], T.Win[0:64, 6144:6304]))
-    need("v", kT2, kK16)
-    kThr = done("v", V.tensor_scalar(T.thr[:, :], T.k16[:, :], T.t2[:, 0:1], None, A.add))
     o2 = done("s", Sc.activation(T.OB[64:128, 160:512], T.Win[0:64, 6304:6656], F.Copy))
     need("v", o1, o2)
     kCum = done("v", V.tensor_tensor_scan(T.CW[:, 16:528], T.Win[:, 4096:4608], T.OB[:, :], 0.0, A.add, A.add))
@@ -160,7 +154,6 @@ def rank_program(g, core, T, topo):
     c1 = done("s", Sc.activation(T.J1[:, :], T.CW[:, 16:528], F.Sign, bias=T.thr[:, 1:2], scale=-1.0, accum_out=T.LR[:, 29:30]))
     need("v", kCum, kThr)
     kJ2 = done("v", V.tensor_scalar(T.J2[:, :], T.CW[:, 16:528], T.thr[:, 2:3], None, A.is_lt))
-    z3 = done("v", V.memset(T.LR[:, 31:32], 0.0))
     need("v", kJ2)
     c2 = done("v", V.tensor_reduce(T.LR[:, 30:31], T.J2[:, :], AxisListType.X, A.add))
     sent = [0]
@@ -193,7 +186,10 @@ def rank_program(g, core, T, topo):
                                           srcs=[T.LR[:, 28:32]], dsts=[T.LR[:, 4 * i:4 * i + 4] for i in range(7)])], local_sem=S.out)
     nla = 7 * sent[0]
 
-    need("v", kGsh)
+    need("v", ("lw", 64))
+    done("v", V.tensor_copy(T.off0[0:64, :], T.Lw[0:64, :]))
+    kOff0 = done("v", V.tensor_copy(T.off0[64:128, :], T.Lw[0:64, :]))
+    need("v", kOff0)
     ko1 = done("v", V.tensor_scalar(T.o1[:, :], T.off0[:, :], T.gsh[:, 0:1], 4608.0, A.add, A.min))
     kq0 = done("v", V.tensor_copy(T.q0[:, :], T.off0[:, :]))
     need("v", ko1)
@@ -212,19 +208,16 @@ def rank_program(g, core, T, topo):
 
     a, b = divmod(r, 2)
     ra = slice(32 * a, 32 * a + 32)
-    hb = slice(16 * b, 16 * b + 16)
     need("v", ("la", nla), c1, c2)
     kX1 = done("v", V.transpose(T.X1[ra, :], T.LR[ra, :]))
     need("v", kX1)
-    need("s", kX1)
-    todo = [(d, u) for d in range(4) for u in range(2) if (d, u) != (a, b)]
-    kcs = kcv = None
-    for n, (d, u) in enumerate(todo):
-        o = T.X1[32 * d:32 * d + 32, 16 * u:16 * u + 16]
-        if n < 2:
-            kcs = done("s", Sc.activation(o, T.X1[ra, hb], F.Copy))
-        else:
-            kcv = done("v", V.tensor_copy(o, T.X1[ra, hb]))
+    kXd = done("v", V.tensor_copy(T.X1[ra, 16 - 16 * b:32 - 16 * b], T.X1[ra, 16 * b:16 * b + 16]))
+    need("v", kXd)
+    need("s", kXd)
+    todo = [slice(32 * d, 32 * d + 32) for d in range(4) if d != a]
+    kcs = done("s", Sc.activation(T.X1[todo[0], :], T.X1[ra, :], F.Copy))
+    for o in todo[1:]:
+        kcv = done("v", V.tensor_copy(T.X1[o, :], T.X1[ra, :]))
     need("v", kcs, kcv)
     kX3 = done("v", V.transpose(T.X3[:, :], T.X1[:, :]))
     need("v", kX3)
@@ -325,4 +318,4 @@ def rank_program(g, core, T, topo):
         queues[qn].dma_start(T.y[:, 256 + 16 * lo:256 + 16 * hi], T.ys[:, 16 * lo:16 * hi]).then_inc(S.ly, 16)
 
     need("g", ("out", sent[0]), ("v", cnt["v"]), ("s", cnt["s"]), ("g", cnt["g"]), ("t", cnt["t"]))
-    need("g", ("lw", 64), ("lc", 64), ("lx", 16), ("lv", 16), ("ly", 64), ("la", nla), ("a0", 32), ("a1", 32), ("a2", 32))
+    need("g", ("ld", 64), ("lz", 32), ("lw", 64), ("lx", 16), ("lv", 16), ("ly", 64), ("la", nla), ("a0", 32), ("a1", 32), ("a2", 32))

from concourse.bass import DstId, RemoteDMATransfer
from concourse.mybir import dt, AluOpType, AxisListType, ActivationFunctionType

A = AluOpType
F = ActivationFunctionType
CAP = 48
PL = 528
BIG = 8192.0


def sb(kind, **widths):
    return {k: ("sbuf", [128, n], kind) for k, n in widths.items()}


SCRATCH = {
    **sb("int32", Lw=32, D=16, Ei=32, pid=1, p4=1, q0=32, q1=32, q2=32, q3=32),
    **sb("uint16", off0=32, EO=32, off1=16, O=24, OO=4, OP=64, FO=32),
    **sb("float32", Cf=4, Cb=4, Dc=16, X=512, R=512, row=128, bt=1, p4f=1, t2=1, gsh=1, did=4, k16=4, thr=4, K=4, G=40, TG=32,
         J0=512, J1=512, LR=32, X1=32, X3=32, Z=384, yv=256, ys=256, o1=32, q4=32, xa=32, xb=32, xc=32, xd=32, xe=32, xf=32),
    **sb("bfloat16", E0=512, E1=384, E2=256, E3=128, NB=2048, MK=640, ones=256, Win=8704, OB=512, CW=544, J2=512,
         x0=2048, XP=4 * PL, wt=512, H=1344, HO=512, Pr=1024, PT=1024),
    **sb("float8_e4m3fn_x4", Q=256, Q2=128, QO=128, QW=128, CR=336),
    **sb("uint8", SQ=256, S2=128, SO=128, SW=128, SR=336),
    "pa": ("psum", [128, 512], "float32"), "pb": ("psum", [128, 512], "float32"), "po": ("psum", [128, 512], "float32"),
}
SEMAPHORES = ["v", "s", "g", "t", "ld", "lz", "lw", "lx", "lv", "ly", "la", "a0", "a1", "a2", "out"]


def rank_program(g, core, T, topo):
    r = T.rank_of(core)
    if r is None:
        return
    N = len(T.cores)
    S = T.sem
    cnt = {"v": 0, "s": 0, "g": 0, "t": 0}
    queues = {"v": g.vector, "s": g.scalar, "g": g, "t": g.tensor, "y": g.sync}
    waited = {}

    def need(qn, *toks):
        for name, n in toks:
            if waited.get((qn, name), 0) < n:
                waited[(qn, name)] = n
                queues[qn].wait_ge(S[name], n)

    def done(qn, ins):
        ins.then_inc(S[qn], 1)
        cnt[qn] += 1
        return (qn, cnt[qn])

    V, Sc = g.vector, g.scalar

    def iota(ap, n, base=0, cm=0, step=1):
        return done("g", g.iota(ap, [[step, n]], base, cm, allow_small_or_imprecise_dtypes=True))

    for e in range(4):
        q = g.sync if e % 2 == 0 else g.scalar
        q.dma_start(T.D[32 * e:32 * e + 32, :], T.want[:, :]).then_inc(S.ld, 16)

    kEi = done("g", g.iota(T.Ei[:, :], [[1, 16], [0, 2]], 0, 0))
    kPid = done("g", g.iota(T.pid[:, :], [[1, 1]], 0, 1))
    kBt = iota(T.bt[:, :], 1, int(BIG), int(BIG))
    kRow = iota(T.row[:, :], 128)
    kK16 = iota(T.k16[:, :], 4, 0, 1, 16)
    kDid = iota(T.did[:, :], 4, 4096, 4)
    kOnes = iota(T.ones[:, :], 256, 1, step=0)
    kWin2 = iota(T.Win[:, 6144:6656], 512, step=0)
    iota(T.CW[:, 0:16], 16, step=0)
    kCz = iota(T.CW[:, 528:544], 16, step=0)
    kMz = done("v", V.memset(T.MK[:, 128:640], 0.0))
    need("v", kEi)
    kEO = done("v", V.tensor_copy(T.EO[:, :], T.Ei[:, :]))
    need("v", kPid)
    kP4 = done("v", V.tensor_scalar(T.p4[:, :], T.pid[:, :], 4, None, A.arith_shift_right))
    need("v", kP4)
    kP4f = done("v", V.tensor_copy(T.p4f[:, :], T.p4[:, :]))
    z3 = done("v", V.memset(T.LR[:, 31:32], 0.0))
    need("y", kMz)
    for lo in (4096, 2048):
        g.sync.dma_start(T.Win[:, lo:lo + 512], T.MK[:, 128:640]).then_inc(S.lz, 16)
    for h in range(4):
        g.sync.dma_start(T.Lw[16 * h:16 * h + 16, :], T.want[:, :]).then_inc(S.lw, 16)
    g.sync.dma_start(T.x0[:, :], T.x[:, :]).then_inc(S.lx, 16)
    g.sync.dma_start(T.wt[:, :], T.w[:, :]).then_inc(S.lv, 16)

    need("v", ("ld", 64))
    kDc = done("v", V.tensor_scalar(T.Dc[:, :], T.D[:, :], BIG, None, A.mult))
    need("v", kEO)
    kXv = done("v", V.tensor_scalar(T.X[:, 0:320], T.D[:, 0:16].indirect(T.EO[:, 0:20]), BIG, None, A.mult))
    need("s", kDc, kEO)
    kXs = done("s", Sc.activation(T.X[:, 320:512], T.Dc[:, 0:16].indirect(T.EO[:, 20:32]), F.Copy))
    need("s", kBt, kRow)
    kTri = done("s", Sc.activation(T.MK[:, 0:128], T.row[:, :], F.Relu, bias=T.bt[:, 0:1], scale=-BIG))
    for e in range(4):
        h = slice(32 * e, 32 * e + 32)
        kCb = done("s", Sc.activation(T.Cb[h, :], T.Dc[h, e:16:4], F.Copy))
    need("v", kXv, kXs)
    kR1 = done("v", V.transpose(T.R[:, 256:512], T.X[:, 256:512]))
    kR0 = done("v", V.transpose(T.R[:, 0:256], T.X[:, 0:256]))
    E = [T.E0, T.E1, T.E2, T.E3]
    need("s", kR1, kCb)
    kS, kE = {}, {}
    for k in (3, 2, 1, 0):
        lo = max(128 * k, 256)
        kS[k] = done("s", Sc.activation(E[k][:, lo - 128 * k:512 - 128 * k], T.R[:, lo:512], F.Abs, bias=T.Cb[:, k:k + 1], scale=-1.0))
    kC = done("s", Sc.activation(T.Cf[:, :], T.Cb[:, :], F.Copy, scale=1.0 / BIG))
    need("s", kP4f)
    kGsh = done("s", Sc.activation(T.gsh[:, :], T.p4f[:, :], F.Identity, bias=4096.0, scale=-512.0))
    kT2 = done("s", Sc.activation(T.t2[:, :], T.p4f[:, :], F.Identity, bias=0.5, scale=-16.0))
    need("v", kR0, kCb)
    for k in (1, 0):
        kE[k] = done("v", V.tensor_scalar(E[k][:, 0:256 - 128 * k], T.R[:, 128 * k:256], T.Cb[:, k:k + 1], BIG, A.not_equal, A.mult))
    need("v", kTri, kMz)
    for k in (3, 2, 1, 0):
        need("v", kS[k])
        if k < 2:
            need("v", kE[k])
        kN = done("v", V.tensor_tensor_scan(T.NB[:, 640 * k:512 * k + 512], E[k][:, :], T.MK[:, 0:512 - 128 * k], BIG, A.min, A.max))
    need("v", kN, kDid, kC)
    kK = done("v", V.tensor_tensor(T.K[:, :], T.did[:, :], T.NB[:, 511:2048:512], A.subtract))
    need("v", kK)
    e1 = done("v", V.tensor_tensor(T.G[:, 0:4], T.K[:, :], T.Cf[:, :], A.max))
    e2 = done("v", V.tensor_tensor(T.G[:, 12:16], T.K[:, :], T.Cf[:, :], A.max))
    need("v", e1)
    need("s", e1)
    done("v", V.tensor_copy(T.G[0:64, 4:8], T.G[64:128, 0:4]))
    a1 = done("v", V.tensor_copy(T.G[0:64, 8:12], T.G[64:128, 0:4]))
    done("s", Sc.activation(T.G[64:128, 4:8], T.G[0:64, 0:4], F.Copy))
    b1 = done("s", Sc.activation(T.G[64:128, 8:12], T.G[0:64, 0:4], F.Copy))
    need("v", a1, b1, e2)
    need("s", a1, b1, e2)
    done("v", V.tensor_copy(T.G[0:32, 16:32], T.G[32:64, 0:16]))
    done("v", V.tensor_copy(T.G[32:64, 16:32], T.G[0:32, 0:16]))
    a2 = done("v", V.tensor_copy(T.G[:, 32:40], T.G[:, 0:8]))
    done("s", Sc.activation(T.G[64:96, 16:32], T.G[96:128, 0:16], F.Copy))
    b2 = done("s", Sc.activation(T.G[96:128, 16:32], T.G[64:96, 0:16], F.Copy))
    need("s", kT2, kK16)
    kThr = done("s", Sc.activation(T.thr[:, :], T.k16[:, :], F.Identity, bias=T.t2[:, 0:1]))
    need("v", a2, b2)
    kTG = done("v", V.transpose(T.TG[:, :], T.G[:, 8:40]))
    need("v", kTG, kGsh)
    done("v", V.tensor_scalar(T.off1[0:64, :], T.TG[0:64, 0:16], T.gsh[0:64, 0:1], None, A.add))
    kO1 = done("v", V.tensor_scalar(T.off1[64:128, :], T.TG[64:128, 16:32], T.gsh[64:128, 0:1], None, A.add))
    need("v", kO1, kOnes, kWin2, ("lz", 32))
    kSc = done("v", V.tensor_copy(T.Win[:, 0:8704].indirect(T.off1[:, 0:16]), T.ones[:, :]))
    need("v", kSc)
    need("s", kSc)
    done("v", V.tensor_copy(T.OB[0:64, :], T.Win[64:128, 2048:2560]))
    o1 = done("v", V.tensor_copy(T.OB[64:128, 0:160], T.Win[0:64, 6144:6304]))
    o2 = done("s", Sc.activation(T.OB[64:128, 160:512], T.Win[0:64, 6304:6656], F.Copy))
    need("v", o1, o2)
    kCum = done("v", V.tensor_tensor_scan(T.CW[:, 16:528], T.Win[:, 4096:4608], T.OB[:, :], 0.0, A.add, A.add))
    need("s", kCum, kThr)
    done("s", Sc.activation(T.J0[:, :], T.CW[:, 16:528], F.Sign, bias=T.thr[:, 0:1], scale=-1.0, accum_out=T.LR[:, 28:29]))
    c1 = done("s", Sc.activation(T.J1[:, :], T.CW[:, 16:528], F.Sign, bias=T.thr[:, 1:2], scale=-1.0, accum_out=T.LR[:, 29:30]))
    need("v", kCum, kThr)
    kJ2 = done("v", V.tensor_scalar(T.J2[:, :], T.CW[:, 16:528], T.thr[:, 2:3], None, A.is_lt))
    need("v", kJ2)
    c2 = done("v", V.tensor_reduce(T.LR[:, 30:31], T.J2[:, :], AxisListType.X, A.add))
    sent = [0]

    def mask(dst, pick):
        es = topo.engines(core, dst)
        m = 0
        for j in pick(len(es)):
            m |= 1 << es[j]
            sent[0] += 1
        return m

    def at(dst):
        rid, pid, _ = topo.addr(dst)
        return DstId(rid=rid, pnc=pid)

    def fused(items):
        tr = []
        for d, src, out, sem, pick in items:
            c = T.cores[d]
            tr.append(RemoteDMATransfer(dst_ids=[at(c)], dma_engine_mask=mask(c, pick), remote_sem=sem, src=src, dst=out))
        g.remote_dma_fused(tr, local_sem=S.out)

    def every(i, n):
        return lambda ne: range(i, ne, n)

    need("g", c1, z3, c2)
    to = [T.cores[(r - 1 - i) % N] for i in range(7)]
    g.remote_dma_fused([RemoteDMATransfer(dst_ids=[at(c) for c in to], dma_engine_mask=mask(to[0], every(0, 1)), remote_sem=S.la,
                                          srcs=[T.LR[:, 28:32]], dsts=[T.LR[:, 4 * i:4 * i + 4] for i in range(7)])], local_sem=S.out)
    nla = 7 * sent[0]

    need("v", ("lw", 64))
    done("v", V.tensor_copy(T.off0[0:64, :], T.Lw[0:64, :]))
    kOff0 = done("v", V.tensor_copy(T.off0[64:128, :], T.Lw[0:64, :]))
    need("v", kOff0)
    ko1 = done("v", V.tensor_scalar(T.o1[:, :], T.off0[:, :], T.gsh[:, 0:1], 4608.0, A.add, A.min))
    kq0 = done("v", V.tensor_copy(T.q0[:, :], T.off0[:, :]))
    need("v", ko1)
    done("v", V.tensor_scalar(T.OP[:, 0:64:2], T.o1[:, :], 4095.0, -4080.0, A.max, A.add))
    kOP = done("v", V.tensor_scalar(T.OP[:, 1:64:2], T.o1[:, :], 4095.0, -4080.0, A.max, A.add))
    need("v", ("lx", 16))
    for t in (0, 1, 2):
        done("v", V.tensor_copy(T.XP[:, PL * t:PL * t + 512], T.x0[:, t:2048:4]))
    kPad = done("v", V.memset(T.XP[:, 512:4 * PL:PL], 0.0))
    need("s", ("lx", 16))
    kPlS = done("s", Sc.activation(T.XP[:, PL * 3:PL * 3 + 512], T.x0[:, 3:2048:4], F.Copy))
    need("s", kOP, kCz, kCum)
    kPs = done("s", Sc.activation(T.Pr[:, 384:1024], T.CW[:, 0:544].indirect(T.OP[:, 24:64]), F.Copy))
    need("v", kOP, kCz, kCum)
    kPv = done("v", V.tensor_copy(T.Pr[:, 0:384], T.CW[:, 0:544].indirect(T.OP[:, 0:24])))

    a, b = divmod(r, 2)
    ra = slice(32 * a, 32 * a + 32)
    need("v", ("la", nla), c1, c2)
    kX1 = done("v", V.transpose(T.X1[ra, :], T.LR[ra, :]))
    need("v", kX1)
    kXd = done("v", V.tensor_copy(T.X1[ra, 16 - 16 * b:32 - 16 * b], T.X1[ra, 16 * b:16 * b + 16]))
    need("v", kXd)
    need("s", kXd)
    todo = [slice(32 * d, 32 * d + 32) for d in range(4) if d != a]
    kcs = done("s", Sc.activation(T.X1[todo[0], :], T.X1[ra, :], F.Copy))
    for o in todo[1:]:
        kcv = done("v", V.tensor_copy(T.X1[o, :], T.X1[ra, :]))
    need("v", kcs, kcv)
    kX3 = done("v", V.transpose(T.X3[:, :], T.X1[:, :]))
    need("v", kX3)
    done("v", V.tensor_scalar(T.O[:, 0:21:3], T.X3[:, 0:28:4], 0.5, 256.0, A.mult, A.add))
    done("v", V.tensor_scalar(T.O[:, 1:21:3], T.X3[:, 1:28:4], 0.5, 256.0, A.mult, A.add))
    kO = done("v", V.tensor_copy(T.O[:, 2:21:3], T.X3[:, 2:28:4]))

    def pick(h, o, t, lo, hi):
        return h[:, 64 * lo + t:64 * hi:4], T.XP[:, PL * t:PL * t + 513].indirect(o[:, lo:hi])

    part = [(0, 8), (8, 16), (16, 21)]
    need("s", kO, kPlS, kPad)
    kh = []
    for lo, hi in part:
        for t in (2, 3):
            k = done("s", Sc.activation(*pick(T.H, T.O, t, lo, hi), F.Copy))
        kh.append(k)
    need("v", kO, kPlS, kPad)
    eng = {2: [every(0, 2), every(1, 2)], 3: [every(0, 2), every(1, 4), every(3, 4)]}
    flip = {2: [every(1, 2), every(0, 2)], 3: [every(1, 2), every(0, 4), every(2, 4)]}
    kv = {}
    for n, ids in enumerate(((0, 1), (2, 3, 4), (5, 6))):
        for m, t in ((n, 0), (n, 1), (n + 1, 0)):
            if m < 3 and (m, t) not in kv:
                kv[m, t] = done("v", V.tensor_copy(*pick(T.H, T.O, t, *part[m])))
        q, p, lo, c0 = (T.Q, T.SQ, 128 * n, 0) if n < 2 else (T.Q2, T.S2, 0, 208)
        need("v", kv[n, 0], kv[n, 1], kh[n])
        kq = done("v", V.quantize_mx(q[:, lo:lo + 128], p[:, lo:lo + 128], T.H[:, 4 * (lo + c0):4 * (lo + c0) + 512]))
        need("g", kq)
        to = [((r + 1 + i) % N, slice(CAP * i - c0, CAP * i - c0 + CAP), slice(CAP * i, CAP * i + CAP)) for i in ids]
        sem = S["a%d" % n]
        fused([(d, q[:, c].bitcast(dt.uint8), T.CR[:, e].bitcast(dt.uint8), sem, m) for (d, c, e), m in zip(to, eng[len(to)])])
        fused([(d, p[:, c], T.SR[:, e], sem, m) for (d, c, e), m in zip(to, flip[len(to)])])
    done("v", V.tensor_scalar(T.OO[:, 0:2], T.X3[:, 28:30], 0.5, 256.0, A.mult, A.add))
    kOO = done("v", V.tensor_copy(T.OO[:, 2:3], T.X3[:, 30:31]))
    need("s", kOO)
    for t in range(4):
        kHo = done("s", Sc.activation(*pick(T.HO, T.OO, t, 0, 3), F.Copy))
    need("v", ("lv", 16))
    kW = done("v", V.quantize_mx(T.QW[:, :], T.SW[:, :], T.wt[:, :]))

    need("v", kPs, kPv)
    kPT = done("v", V.transpose(T.PT[:, :], T.Pr[:, :]))
    kHz = done("v", V.memset(T.HO[:, 192:512], 0.0))
    need("v", kq0)
    kq1 = done("v", V.tensor_scalar(T.q1[:, :], T.q0[:, :], 9, None, A.arith_shift_right))
    need("v", kPT)
    kxa = done("v", V.tensor_tensor(T.xa[:, :], T.PT[:, 0:1024:32], T.PT[:, 16:1024:32], A.add))
    need("v", kxa)
    need("s", kxa)
    x1 = done("v", V.tensor_copy(T.xb[0:64, :], T.xa[64:128, :]))
    x2 = done("s", Sc.activation(T.xb[64:128, :], T.xa[0:64, :], F.Copy))
    need("v", kq1)
    kq2 = done("v", V.tensor_scalar(T.q2[:, :], T.q1[:, :], -1.0, float(r + 7), A.mult, A.add))
    need("v", kHo, kHz)
    kqo = done("v", V.quantize_mx(T.QO[:, :], T.SO[:, :], T.HO[:, :]))
    need("v", x1, x2)
    kxc = done("v", V.tensor_tensor(T.xc[:, :], T.xa[:, :], T.xb[:, :], A.add))
    need("v", kq2)
    kq3 = done("v", V.tensor_scalar(T.q3[:, :], T.q2[:, :], 7, None, A.bitwise_and))
    need("v", kxc)
    need("s", kxc)
    done("v", V.tensor_copy(T.xd[0:32, :], T.xc[32:64, :]))
    x3 = done("v", V.tensor_copy(T.xd[32:64, :], T.xc[0:32, :]))
    done("s", Sc.activation(T.xd[64:96, :], T.xc[96:128, :], F.Copy))
    x4 = done("s", Sc.activation(T.xd[96:128, :], T.xc[64:96, :], F.Copy))
    need("v", kq3)
    kq4 = done("v", V.tensor_scalar(T.q4[:, :], T.q3[:, :], 48.0, -1.0, A.mult, A.add))
    need("v", kq4)
    kxe = done("v", V.tensor_tensor(T.xe[:, :], T.xc[:, :], T.q4[:, :], A.add))
    need("v", x3, x4, kxe)
    kxf = done("v", V.tensor_tensor(T.xf[:, :], T.xe[:, :], T.xd[:, :], A.add))
    need("v", kxf)
    kFO = done("v", V.tensor_copy(T.FO[:, :], T.xf[:, :]))

    ts = g.tensor
    need("t", kW, kqo)
    m0 = done("t", ts.matmul_mx(T.po[:, 0:128], T.QW[:, :], T.SW[:, :], T.QO[:, :], T.SO[:, :], True, True))
    need("t", ("a0", 32), ("a1", 32))
    m1 = done("t", ts.matmul_mx(T.pa[:, 0:240], T.QW[:, :], T.SW[:, :], T.CR[:, 0:240], T.SR[:, 0:240], True, True))
    need("t", ("a2", 32))
    m2 = done("t", ts.matmul_mx(T.pb[:, 0:128], T.QW[:, :], T.SW[:, :], T.CR[:, 208:336], T.SR[:, 208:336], True, True))

    need("v", m0)
    zo = done("v", V.tensor_copy(T.Z[:, 336:384], T.po[:, 0:48]))
    need("s", m1)
    za = done("s", Sc.activation(T.Z[:, 0:240], T.pa[:, 0:240], F.Copy))
    need("v", m2)
    zb = done("v", V.tensor_copy(T.Z[:, 240:336], T.pb[:, 32:128]))
    need("v", kFO, zo, za, zb)
    need("s", kFO, zo, za, zb)
    for lo, hi, qn in ((0, 6, "y"), (6, 16, "s")):
        ky = done("v", V.tensor_copy(T.yv[:, 16 * lo:16 * hi], T.Z[:, 0:384].indirect(T.FO[:, lo:hi])))
        need("y", ky)
        g.sync.dma_start(T.y[:, 16 * lo:16 * hi], T.yv[:, 16 * lo:16 * hi]).then_inc(S.ly, 16)
        ky = done("s", Sc.activation(T.ys[:, 16 * lo:16 * hi], T.Z[:, 0:384].indirect(T.FO[:, 16 + lo:16 + hi]), F.Copy))
        need(qn, ky)
        queues[qn].dma_start(T.y[:, 256 + 16 * lo:256 + 16 * hi], T.ys[:, 16 * lo:16 * hi]).then_inc(S.ly, 16)

    need("g", ("out", sent[0]), ("v", cnt["v"]), ("s", cnt["s"]), ("g", cnt["g"]), ("t", cnt["t"]))
    need("g", ("ld", 64), ("lz", 32), ("lw", 64), ("lx", 16), ("lv", 16), ("ly", 64), ("la", nla), ("a0", 32), ("a1", 32), ("a2", 32))
